import numpy as np
import ml_dtypes


def mxq(x, axis, fmt="e4m3"):
    dtype, down = {"e4m3": (ml_dtypes.float8_e4m3fn, 7), "e5m2": (ml_dtypes.float8_e5m2, 14)}[fmt]
    v = np.moveaxis(np.asarray(x, np.float32).astype(ml_dtypes.bfloat16).astype(np.float64), axis, -1)
    blocks = v.reshape(v.shape[:-1] + (-1, 32))
    amax = np.abs(blocks).max(-1, keepdims=True)
    byte = np.maximum(np.where(amax > 0, np.frexp(amax)[1] - 1 + 127, 0) - down, 1)
    scale = np.exp2(byte - 127.0)
    codes = (blocks / scale).astype(np.float32).astype(dtype).astype(np.float64)
    return np.moveaxis((codes * scale).reshape(v.shape), -1, axis)


WIDE = False


def mx_kscale(k):
    if not WIDE:
        return np.ones(k)
    levels = np.array([10, -10, 5, -5, 0])
    if k % 512:
        return np.exp2(np.random.permutation(np.resize(levels, k // 32))).repeat(32)
    a = np.empty((k // 512, 16))
    for p in range(k // 512):
        a[p, :8] = np.random.permutation(np.resize(levels, 8))
        for g in range(8):
            far = levels[np.abs(levels - a[p, g]) >= 10]
            a[p, g + 8] = far[np.random.randint(len(far))]
    return np.exp2(a.ravel()).repeat(32)


def f64(x):
    return np.asarray(x).astype(np.float64)


def striped(idx):
    return np.tile(idx.reshape(-1, 16).T, (8, 1)).astype(np.uint16)


def unstriped(offs):
    return offs[:16].T.reshape(-1).astype(np.int64)


E2M1 = np.array([0.0, 0.5, 1.0, 1.5, 2.0, 3.0, 4.0, 6.0, -0.0, -0.5, -1.0, -1.5, -2.0, -3.0, -4.0, -6.0])


def pack_weight(w, fmt):
    k, n = w.shape
    w = f64(np.asarray(w, np.float32).astype(ml_dtypes.bfloat16)).reshape(k // 32, 32, n)
    amax = np.abs(w).max(1)
    if fmt == "e4m3":
        byte = np.frexp(amax)[1] - 1 + 127 - 7
    else:
        mant, ex = np.frexp(amax / 6.0)
        byte = np.where(mant > 0.5, ex, ex - 1) + 127
    byte = np.clip(np.where(amax > 0, byte, 1), 1, 254)
    scaled = (w * np.exp2(127.0 - byte)[:, None, :]).reshape(k, n).astype(np.float32)
    by_word = np.ascontiguousarray(scaled.reshape(k // 512, 128, 4, n).transpose(0, 1, 3, 2))
    if fmt == "e4m3":
        words = by_word.astype(ml_dtypes.float8_e4m3fn).view(np.uint8)
    else:
        c = by_word.astype(ml_dtypes.float4_e2m1fn).view(np.uint8) & 0xF
        words = (c[..., 0::2] | (c[..., 1::2] << 4)).reshape(k // 512, 128, 2 * n)
    return np.ascontiguousarray(words), np.ascontiguousarray(byte.astype(np.uint8).reshape(k // 512, 16, n))


def unpack_weight(words, scales, fmt):
    g, _, n = scales.shape
    words = np.ascontiguousarray(words).reshape(g, 128, n, -1)
    if fmt == "e4m3":
        vals = words.view(ml_dtypes.float8_e4m3fn).astype(np.float64)
    else:
        nib = np.empty((g, 128, n, 4), np.uint8)
        nib[..., 0::2] = words & 0xF
        nib[..., 1::2] = words >> 4
        vals = E2M1[nib]
    vals = vals * np.repeat(np.exp2(scales.astype(np.float64) - 127.0), 8, axis=1)[..., None]
    return vals.transpose(0, 1, 3, 2).reshape(g * 512, n)


def gelu(v):
    return 0.5 * v * (1.0 + np.tanh(np.sqrt(2.0 / np.pi) * (v + 0.044715 * v**3)))


K, K2, T, S, T2, H, N = 1024, 512, 2048, 512, 1024, 1536, 384

def setup_inputs():
    n = np.random.standard_normal
    s = mx_kscale(K)[:, None]
    s2 = mx_kscale(K2)[:, None]
    u = mx_kscale(H)[:, None]
    tab_words, tab_scales = pack_weight(n((K, T)) * s, "e4m3")
    tab2_words, tab2_scales = pack_weight(n((K2, T)) * s2, "e4m3")
    w2_words, w2_scales = pack_weight(1.3 * n((K2, H)) / np.sqrt(K2) / s2 * u.T, "e2m1")
    w4_words, w4_scales = pack_weight(0.6 * n((H, N)) / np.sqrt(H) / u, "e2m1")
    return {
        "tab_words": tab_words, "tab_scales": tab_scales,
        "tab2_words": tab2_words, "tab2_scales": tab2_scales,
        "offs": striped(np.random.permutation(T)[:S]),
        "offs2": striped(np.random.permutation(T)[:S]),
        "offs3": striped(np.random.permutation(T2)[:S]),
        "offs4": striped(np.random.permutation(T2)[:S]),
        "w1": (1.6 * n((K, H)) / np.sqrt(K) / s).astype(np.float32),
        "gain": (1.5 * np.exp(0.3 * n(H))).astype(np.float32),
        "w2_words": w2_words, "w2_scales": w2_scales,
        "wg1": np.exp(0.3 * n((128, S))).astype(np.float32),
        "wg2": np.exp(0.3 * n((128, S))).astype(np.float32),
        "vis": (n((H, T2)) * u).astype(np.float32),
        "w3": (0.6 * n((H, N)) / np.sqrt(H) / u).astype(np.float32),
        "w4_words": w4_words, "w4_scales": w4_scales,
    }

def reference(tab_words, tab_scales, tab2_words, tab2_scales, offs, offs2, offs3, offs4, w1, gain, w2_words, w2_scales, wg1, wg2, vis, w3, w4_words, w4_scales):
    v = unpack_weight(tab_words, tab_scales, "e4m3")[:, unstriped(offs)]
    v2 = unpack_weight(tab2_words, tab2_scales, "e4m3")[:, unstriped(offs2)]
    h1 = np.tanh(mxq(f64(w1), 0, "e4m3").T @ v) * f64(gain)[:, None]
    h2 = unpack_weight(w2_words, w2_scales, "e2m1").T @ v2
    pa = np.zeros((H, T2))
    pa[:, unstriped(offs3)] = np.tile(f64(wg1), (H // 128, 1)) * h1
    pb = np.zeros((H, T2))
    pb[:, unstriped(offs4)] = np.tile(f64(wg2), (H // 128, 1)) * h2
    z = f64(vis) * (1.0 + np.abs(pa)) + pb
    zq = mxq(z, 0, "e4m3")
    y1 = mxq(f64(w3), 0, "e4m3").T @ zq
    y2 = unpack_weight(w4_words, w4_scales, "e2m1").T @ zq
    return y1 * y2

@@ -1,0 +1,326 @@
+from contextlib import ExitStack
+
+import concourse.mybir as mybir
+from concourse.masks import make_identity
+
+K, K2, T, S, T2, H, N = 1024, 512, 2048, 512, 1024, 1536, 384
+FLOPS = 2 * (K * H * S + K2 * H * S + 2 * H * N * T2)
+
+F32 = mybir.dt.float32
+BF16 = mybir.dt.bfloat16
+I32 = mybir.dt.int32
+U32 = mybir.dt.uint32
+U16 = mybir.dt.uint16
+U8 = mybir.dt.uint8
+FP8X4 = mybir.dt.float8_e4m3fn_x4
+FP4X4 = mybir.dt.float4_e2m1fn_x4
+ALU = mybir.AluOpType
+ACT = mybir.ActivationFunctionType
+
+P = 128
+PACK = 4
+K_PASS = P * PACK
+BANK = 512
+TILES = H // P
+R_PASSES = H // K_PASS
+TILES_PER_PASS = K_PASS // P
+K_PASSES = K // K_PASS
+W1_COLS = 256
+W1_CHUNKS = H // W1_COLS
+HALVES = T2 // BANK
+M_BLOCKS = BANK // P
+N_TILES = N // P
+QUADS = 4
+
+
+def tile_list_alert_queue_ranker_kernel(
+    tc, tab_words, tab_scales, tab2_words, tab2_scales, offs, offs2, offs3, offs4,
+    w1, gain, w2_words, w2_scales, wg1, wg2, vis, w3, w4_words, w4_scales, out,
+):
+    nc = tc.nc
+    with ExitStack() as ctx:
+        keep = ctx.enter_context(tc.tile_pool(name="keep", bufs=1))
+        ring = ctx.enter_context(tc.tile_pool(name="ring", bufs=2))
+        psum = ctx.enter_context(tc.psum_pool(name="psum", bufs=1))
+
+        banks = [psum.tile([P, BANK], F32, name=f"bank{i}") for i in range(8)]
+        h1_banks = (banks[0], banks[4])
+        h2_banks = (banks[1], banks[5])
+        sum_banks = ((banks[2], banks[3]), (banks[6], banks[7]))
+        turn_banks = (banks[6], banks[7])
+
+        offs_sb = keep.tile([P, S // 16], U16, name="offs_sb")
+        offs2_sb = keep.tile([P, S // 16], U16, name="offs2_sb")
+        offs3_sb = keep.tile([P, S // 16], U16, name="offs3_sb")
+        offs4_sb = keep.tile([P, S // 16], U16, name="offs4_sb")
+        tab_w = [keep.tile([P, T], I32, name=f"tab_w{a}", align_bytes=64) for a in range(K_PASSES)]
+        tab_s = keep.tile([P, T], U8, name="tab_s", align_bytes=64)
+        tab2_w = keep.tile([P, T], I32, name="tab2_w", align_bytes=64)
+        tab2_s = keep.tile([P, T], U8, name="tab2_s", align_bytes=64)
+        v_w = [keep.tile([P, S], U32, name=f"v_w{a}", align_bytes=64) for a in range(K_PASSES)]
+        v_s = keep.tile([P, S], U8, name="v_s", align_bytes=64)
+        v2_w = keep.tile([P, S], U32, name="v2_w", align_bytes=64)
+        v2_s = keep.tile([P, S], U8, name="v2_s", align_bytes=64)
+        w2_first = keep.tile([P, 2 * P], U8, name="w2_first", align_bytes=64)
+        w2_rest = keep.tile([P, 2 * (H - P)], U8, name="w2_rest", align_bytes=64)
+        w2_s = keep.tile([P, H], U8, name="w2_s", align_bytes=64)
+        w4_w = keep.tile([P, R_PASSES * 2 * N], U8, name="w4_w", align_bytes=64)
+        w4_s = keep.tile([P, R_PASSES * N], U8, name="w4_s", align_bytes=64)
+        w1_q = [keep.tile([P, K_PASSES * W1_COLS], U32, name=f"w1_q{k}", align_bytes=64) for k in range(W1_CHUNKS)]
+        w1_s = [keep.tile([P, K_PASSES * W1_COLS], U8, name=f"w1_s{k}", align_bytes=64) for k in range(W1_CHUNKS)]
+        w3_q = [keep.tile([P, N], U32, name=f"w3_q{b}", align_bytes=64) for b in range(R_PASSES)]
+        w3_s = [keep.tile([P, N], U8, name=f"w3_s{b}", align_bytes=64) for b in range(R_PASSES)]
+        z_q = [[keep.tile([P, BANK], U32, name=f"z_q{b}{h}", align_bytes=64) for h in range(HALVES)] for b in range(R_PASSES)]
+        z_s = [[keep.tile([P, BANK], U8, name=f"z_s{b}{h}", align_bytes=64) for h in range(HALVES)] for b in range(R_PASSES)]
+        wg1_sb = keep.tile([P, S], F32, name="wg1_sb")
+        wg1_abs = keep.tile([P, S], F32, name="wg1_abs")
+        wg2_sb = keep.tile([P, S], F32, name="wg2_sb")
+        gain_rows = keep.tile([P, P], F32, name="gain_rows")
+        gain_sb = keep.tile([P, TILES], F32, name="gain_sb")
+        ident = keep.tile([P, P], F32, name="ident")
+        pages_a = [keep.tile([P, T2], F32, name=f"page_a{i}") for i in range(2)]
+        pages_b = [keep.tile([P, T2], F32, name=f"page_b{i}") for i in range(2)]
+        boosted = keep.tile([P, T2], F32, name="boosted")
+
+        def load_scales(engine, plane, scales):
+            passes = scales.shape[0]
+            for q in range(QUADS):
+                engine.dma_start(
+                    out=plane[32 * q : 32 * q + 4 * passes, :].bitcast(I32),
+                    in_=scales[:, 4 * q : 4 * q + 4, :].bitcast(I32),
+                )
+
+        def table_words(words, a):
+            return words[a].rearrange("p t i -> p (t i)").bitcast(I32)
+
+        for plane in (tab2_s, w2_s, tab_s):
+            nc.vector.memset(plane[:].bitcast(I32), 0)
+        nc.sync.dma_start(offs2_sb[:], offs2)
+        nc.sync.dma_start(out=w2_first[:].bitcast(I32), in_=w2_words[0][:, : 2 * P].bitcast(I32))
+        nc.sync.dma_start(offs4_sb[:], offs4)
+        nc.sync.dma_start(offs_sb[:], offs)
+        nc.sync.dma_start(offs3_sb[:], offs3)
+        nc.sync.dma_start(out=tab2_w[:], in_=table_words(tab2_words, 0))
+        load_scales(nc.sync, tab2_s, tab2_scales)
+        load_scales(nc.sync, w2_s, w2_scales)
+        load_scales(nc.sync, tab_s, tab_scales)
+        nc.sync.dma_start(out=wg2_sb[:], in_=wg2)
+        for page in pages_b:
+            nc.vector.memset(page[:], 0.0)
+        nc.gpsimd.memset(gain_rows[:], 0.0)
+        nc.gpsimd.dma_start(out=gain_rows[:TILES, :], in_=gain.rearrange("(c p) -> c p", p=P))
+        make_identity(nc, ident[:])
+        for page in pages_a:
+            nc.gpsimd.memset(page[:], 0.0)
+        nc.gpsimd.memset(w4_s[:].bitcast(I32), 0)
+
+        w1_raw = {}
+
+        def load_w1(k):
+            raw = ring.tile([P, PACK * K_PASSES * W1_COLS], F32, name="w_raw", tag="w_raw", bufs=3)
+            view = raw[:].rearrange("p (j a c) -> p j a c", j=PACK, a=K_PASSES)
+            for a in range(K_PASSES):
+                nc.sync.dma_start(
+                    out=view[:, :, a, :],
+                    in_=w1[a * K_PASS : (a + 1) * K_PASS, k * W1_COLS : (k + 1) * W1_COLS].rearrange("(p j) c -> p j c", j=PACK),
+                )
+            w1_raw[k] = raw
+
+        w3_raw = {}
+
+        def load_w3(b):
+            raw = ring.tile([P, PACK * N], F32, name="w_raw", tag="w_raw", bufs=3)
+            nc.sync.dma_start(out=raw[:], in_=w3[b * K_PASS : (b + 1) * K_PASS, :].rearrange("(p j) n -> p (j n)", j=PACK))
+            w3_raw[b] = raw
+
+        def quantise_weight(raw, codes, scales):
+            width = raw.shape[1]
+            grouped = ring.tile([P, width], BF16, name="w_bf", tag="w_bf", align_bytes=64)
+            nc.scalar.copy(
+                out=grouped[:].rearrange("p (g i j) -> p g j i", i=4, j=PACK),
+                in_=raw[:].rearrange("p (j g i) -> p g j i", i=4, j=PACK),
+            )
+            nc.vector.quantize_mx(out=codes[:].bitcast(FP8X4), scales=scales[:], in_=grouped[:])
+
+        vis_sb = {}
+
+        def load_vis(c):
+            tile = ring.tile([P, T2], F32, name="vis_sb", tag="vis_sb", bufs=6)
+            nc.sync.dma_start(out=tile[:], in_=vis[c * P : (c + 1) * P, :])
+            vis_sb[c] = tile
+
+        load_w1(0)
+        nc.sync.dma_start(out=tab_w[0][:], in_=table_words(tab_words, 0))
+        nc.sync.dma_start(out=tab_w[1][:], in_=table_words(tab_words, 1))
+        nc.sync.dma_start(out=w2_rest[:].bitcast(I32), in_=w2_words[0][:, 2 * P :].bitcast(I32))
+        nc.sync.dma_start(out=wg1_sb[:], in_=wg1)
+        for k in range(1, 3):
+            load_w1(k)
+
+        h1_sb = {}
+        h2_sb = {}
+
+        def stage_h1(c):
+            bank = h1_banks[c % 2]
+            k, col = divmod(c * P, W1_COLS)
+            for a in range(K_PASSES):
+                cols = slice(a * W1_COLS + col, a * W1_COLS + col + P)
+                nc.tensor.matmul_mx(
+                    out=bank[:], lhsT=w1_q[k][:, cols].bitcast(FP8X4), lhsT_scale=w1_s[k][:, cols],
+                    rhs=v_w[a][:].bitcast(FP8X4), rhs_scale=v_s[4 * a :, :],
+                    start=(a == 0), stop=(a == K_PASSES - 1),
+                )
+            tile = ring.tile([P, S], F32, name="h1_sb", tag="h1_sb", bufs=3)
+            nc.scalar.activation(out=tile[:], in_=bank[:], func=ACT.Tanh)
+            nc.scalar.activation(out=tile[:], in_=tile[:], func=ACT.Abs, scale=gain_sb[:, c : c + 1])
+            h1_sb[c] = tile
+
+        def stage_h2(c):
+            bank = h2_banks[c % 2]
+            words = w2_first[:] if c == 0 else w2_rest[:, 2 * P * (c - 1) : 2 * P * c]
+            nc.tensor.matmul_mx(
+                out=bank[:], lhsT=words.bitcast(FP4X4), lhsT_scale=w2_s[:, c * P : (c + 1) * P],
+                rhs=v2_w[:].bitcast(FP8X4), rhs_scale=v2_s[:], start=True, stop=True,
+            )
+            tile = ring.tile([P, S], F32, name="h2_sb", tag="h2_sb", bufs=3)
+            nc.scalar.copy(out=tile[:], in_=bank[:])
+            h2_sb[c] = tile
+
+        def place_a(c):
+            nc.vector.tensor_tensor(pages_a[c % 2][:].indirect(offs3_sb[:]), h1_sb[c][:], wg1_abs[:], ALU.mult)
+
+        def place_b(c):
+            nc.vector.tensor_tensor(pages_b[c % 2][:].indirect(offs4_sb[:]), h2_sb[c][:], wg2_sb[:], ALU.mult)
+
+        z_t = {}
+
+        def combine(c):
+            b, quad = divmod(c, TILES_PER_PASS)
+            last = c == TILES - 1
+
+            def turn(src, h, mb, start, stop):
+                nc.tensor.matmul(
+                    sum_banks[c % 2][h][:, mb * P : (mb + 1) * P], lhsT=src[:, h * BANK + mb * P : h * BANK + (mb + 1) * P],
+                    rhs=ident[:], is_transpose=True, start=start, stop=stop,
+                )
+
+            if last:
+                for h in range(HALVES):
+                    for mb in range(M_BLOCKS):
+                        turn(pages_b[c % 2], h, mb, mb == 0, False)
+            for cols in (slice(0, BANK), slice(BANK, T2)) if last else (slice(0, T2),):
+                nc.vector.scalar_tensor_tensor(
+                    out=boosted[:, cols], in0=pages_a[c % 2][:, cols], scalar=1.0, in1=vis_sb[c][:, cols], op0=ALU.add, op1=ALU.mult
+                )
+            for h in range(HALVES):
+                if quad == 0:
+                    z_t[h] = ring.tile([P, M_BLOCKS * K_PASS], BF16, name=f"z_t{h}", tag=f"z_t{h}")
+                bank = sum_banks[c % 2][h]
+                for mb in range(M_BLOCKS):
+                    if last:
+                        turn(boosted, h, mb, False, mb == M_BLOCKS - 1)
+                    else:
+                        turn(boosted, h, mb, True, False)
+                        turn(pages_b[c % 2], h, mb, False, True)
+                copy = nc.vector.tensor_copy if last and h == 1 else nc.scalar.copy
+                copy(
+                    out=z_t[h][:].rearrange("m (mb u t q e) -> m mb u t q e", mb=M_BLOCKS, u=2, t=TILES_PER_PASS, e=2)[:, :, :, quad, :, :],
+                    in_=bank[:].rearrange("m (mb q u e) -> m mb u q e", mb=M_BLOCKS, u=2, e=2),
+                )
+
+        def quantise_z(b):
+            for h in range(HALVES):
+                words = z_t[h][:].bitcast(F32).rearrange("m (mb u p) -> m mb u p", mb=M_BLOCKS, u=2)
+                grouped = ring.tile([P, BANK * PACK], BF16, name="z_bf", tag="z_bf", align_bytes=64)
+                pairs = grouped[:].bitcast(F32).rearrange("p (m u) -> p m u", u=2)
+                for i, bank in enumerate(turn_banks):
+                    for u in range(2):
+                        for j in range(2):
+                            nc.tensor.transpose(bank[:, (2 * u + j) * P : (2 * u + j + 1) * P], words[:, 2 * i + j, u, :], ident[:])
+                    copy = nc.vector.tensor_copy if b == R_PASSES - 1 and i == 1 else nc.scalar.copy
+                    copy(out=pairs[:, 2 * i * P : 2 * (i + 1) * P, :], in_=bank[:].rearrange("p (u m) -> p m u", u=2))
+                nc.vector.quantize_mx(out=z_q[b][h][:].bitcast(FP8X4), scales=z_s[b][h][:], in_=grouped[:])
+
+        def read_queue(pair, n, h, passes):
+            for b in passes:
+                col = b * N + n * P
+                nc.tensor.matmul_mx(
+                    out=pair[1][:], lhsT=w4_w[:, 2 * col : 2 * (col + P)].bitcast(FP4X4), lhsT_scale=w4_s[:, col : col + P],
+                    rhs=z_q[b][h][:].bitcast(FP8X4), rhs_scale=z_s[b][h][:], start=(b == 0), stop=(b == R_PASSES - 1),
+                )
+            for b in passes:
+                nc.tensor.matmul_mx(
+                    out=pair[0][:], lhsT=w3_q[b][:, n * P : (n + 1) * P].bitcast(FP8X4), lhsT_scale=w3_s[b][:, n * P : (n + 1) * P],
+                    rhs=z_q[b][h][:].bitcast(FP8X4), rhs_scale=z_s[b][h][:], start=(b == 0), stop=(b == R_PASSES - 1),
+                )
+
+        def finish(pair, n, h):
+            y2 = ring.tile([P, BANK], F32, name="y2", tag="y2")
+            nc.scalar.copy(out=y2[:], in_=pair[1][:])
+            res = ring.tile([P, BANK], F32, name="res", tag="res", bufs=3)
+            nc.vector.tensor_tensor(res[:], pair[0][:], y2[:], ALU.mult)
+            nc.sync.dma_start(out=out[n * P : (n + 1) * P, h * BANK : (h + 1) * BANK], in_=res[:])
+
+        nc.vector.tensor_copy(v2_s[:], tab2_s[:].indirect(offs2_sb[:]))
+        nc.vector.tensor_copy(v2_w[:], tab2_w[:].bitcast(U32).indirect(offs2_sb[:]))
+        stage_h2(0)
+        nc.vector.tensor_copy(v_s[:], tab_s[:].indirect(offs_sb[:]))
+        place_b(0)
+        quantise_weight(w1_raw[0], w1_q[0], w1_s[0])
+        for a in range(K_PASSES):
+            nc.vector.tensor_copy(v_w[a][:], tab_w[a][:].bitcast(U32).indirect(offs_sb[:]))
+        nc.tensor.transpose(banks[6][:, :P], gain_rows[:], ident[:])
+        nc.scalar.copy(out=gain_sb[:], in_=banks[6][:, :TILES])
+        nc.scalar.activation(out=wg1_abs[:], in_=wg1_sb[:], func=ACT.Abs)
+        stage_h1(0)
+        stage_h2(1)
+        stage_h1(1)
+        place_b(1)
+        for k in range(1, W1_CHUNKS):
+            quantise_weight(w1_raw[k], w1_q[k], w1_s[k])
+            if k + 2 < W1_CHUNKS:
+                load_w1(k + 2)
+        for c in range(3):
+            load_vis(c)
+        for b in range(R_PASSES):
+            load_w3(b)
+        nc.sync.dma_start(
+            out=w4_w[:].bitcast(I32).rearrange("p (a n) -> p a n", a=R_PASSES),
+            in_=w4_words.bitcast(I32).rearrange("a p n -> p a n"),
+        )
+        for q in range(QUADS):
+            nc.sync.dma_start(
+                out=w4_s[32 * q : 32 * q + 4, :].bitcast(I32).rearrange("r (a n) -> r a n", a=R_PASSES),
+                in_=w4_scales[:, 4 * q : 4 * q + 4, :].bitcast(I32).rearrange("a r n -> r a n"),
+            )
+        for c in range(3, 6):
+            load_vis(c)
+        place_a(0)
+
+        held_pairs = ((banks[4], banks[5]), (banks[0], banks[1]), (banks[2], banks[3]))
+        for c in range(TILES):
+            if c + 2 < TILES:
+                stage_h1(c + 2)
+                stage_h2(c + 2)
+            if c + 1 < TILES:
+                place_a(c + 1)
+            if c == TILES - 1:
+                for n in range(N_TILES):
+                    read_queue(held_pairs[n], n, 0, range(R_PASSES - 1))
+            combine(c)
+            if c + 6 < TILES:
+                load_vis(c + 6)
+            if 1 <= c + 1 < TILES and c >= 1:
+                place_b(c + 1)
+            if c % TILES_PER_PASS == TILES_PER_PASS - 1:
+                quantise_z(c // TILES_PER_PASS)
+            if 4 <= c < 4 + R_PASSES:
+                quantise_weight(w3_raw[c - 4], w3_q[c - 4], w3_s[c - 4])
+
+        for n in range(N_TILES):
+            read_queue(held_pairs[n], n, 0, [R_PASSES - 1])
+            finish(held_pairs[n], n, 0)
+        late_pairs = (turn_banks, held_pairs[0], held_pairs[1])
+        for n in range(N_TILES):
+            read_queue(late_pairs[n], n, 1, range(R_PASSES))
+            finish(late_pairs[n], n, 1)

@@ -31,6 +31,7 @@ HALVES = T2 // BANK
 M_BLOCKS = BANK // P
 N_TILES = N // P
 QUADS = 4
+HEAD_TILES = 2
 
 
 def tile_list_alert_queue_ranker_kernel(
@@ -73,14 +74,12 @@ def tile_list_alert_queue_ranker_kernel(
         z_q = [[keep.tile([P, BANK], U32, name=f"z_q{b}{h}", align_bytes=64) for h in range(HALVES)] for b in range(R_PASSES)]
         z_s = [[keep.tile([P, BANK], U8, name=f"z_s{b}{h}", align_bytes=64) for h in range(HALVES)] for b in range(R_PASSES)]
         wg1_sb = keep.tile([P, S], F32, name="wg1_sb")
-        wg1_abs = keep.tile([P, S], F32, name="wg1_abs")
         wg2_sb = keep.tile([P, S], F32, name="wg2_sb")
         gain_rows = keep.tile([P, P], F32, name="gain_rows")
         gain_sb = keep.tile([P, TILES], F32, name="gain_sb")
         ident = keep.tile([P, P], F32, name="ident")
         pages_a = [keep.tile([P, T2], F32, name=f"page_a{i}") for i in range(2)]
         pages_b = [keep.tile([P, T2], F32, name=f"page_b{i}") for i in range(2)]
-        boosted = keep.tile([P, T2], F32, name="boosted")
 
         def load_scales(engine, plane, scales):
             passes = scales.shape[0]
@@ -172,6 +171,7 @@ def tile_list_alert_queue_ranker_kernel(
                 )
             tile = ring.tile([P, S], F32, name="h1_sb", tag="h1_sb", bufs=3)
             nc.scalar.activation(out=tile[:], in_=bank[:], func=ACT.Tanh)
+            nc.gpsimd.tensor_tensor(tile[:], tile[:], wg1_sb[:], ALU.mult)
             nc.scalar.activation(out=tile[:], in_=tile[:], func=ACT.Abs, scale=gain_sb[:, c : c + 1])
             h1_sb[c] = tile
 
@@ -184,44 +184,51 @@ def tile_list_alert_queue_ranker_kernel(
             )
             tile = ring.tile([P, S], F32, name="h2_sb", tag="h2_sb", bufs=3)
             nc.scalar.copy(out=tile[:], in_=bank[:])
+            if c >= HEAD_TILES:
+                nc.gpsimd.tensor_tensor(tile[:], tile[:], wg2_sb[:], ALU.mult)
             h2_sb[c] = tile
 
         def place_a(c):
-            nc.vector.tensor_tensor(pages_a[c % 2][:].indirect(offs3_sb[:]), h1_sb[c][:], wg1_abs[:], ALU.mult)
+            nc.vector.tensor_copy(pages_a[c % 2][:].indirect(offs3_sb[:]), h1_sb[c][:])
 
         def place_b(c):
-            nc.vector.tensor_tensor(pages_b[c % 2][:].indirect(offs4_sb[:]), h2_sb[c][:], wg2_sb[:], ALU.mult)
+            if c >= HEAD_TILES:
+                nc.vector.tensor_copy(pages_b[c % 2][:].indirect(offs4_sb[:]), h2_sb[c][:])
+            else:
+                nc.vector.tensor_tensor(pages_b[c % 2][:].indirect(offs4_sb[:]), h2_sb[c][:], wg2_sb[:], ALU.mult)
 
         z_t = {}
+
+        boost = {}
+
+        def scale_vis(c):
+            tile = ring.tile([P, T2], F32, name="boost", tag="boost")
+            if c == TILES - 1:
+                nc.vector.scalar_tensor_tensor(
+                    out=tile[:], in0=pages_a[c % 2][:], scalar=1.0, in1=vis_sb[c][:], op0=ALU.add, op1=ALU.mult
+                )
+            else:
+                for h in range(HALVES):
+                    cols = slice(h * BANK, (h + 1) * BANK)
+                    nc.gpsimd.tensor_tensor(tile[:, cols], pages_a[c % 2][:, cols], vis_sb[c][:, cols], ALU.mult)
+            boost[c] = tile
 
         def combine(c):
             b, quad = divmod(c, TILES_PER_PASS)
             last = c == TILES - 1
-
-            def turn(src, h, mb, start, stop):
-                nc.tensor.matmul(
-                    sum_banks[c % 2][h][:, mb * P : (mb + 1) * P], lhsT=src[:, h * BANK + mb * P : h * BANK + (mb + 1) * P],
-                    rhs=ident[:], is_transpose=True, start=start, stop=stop,
-                )
-
-            if last:
+            terms = (boost[c], pages_b[c % 2]) if last else (vis_sb[c], boost[c], pages_b[c % 2])
+            for i, term in enumerate(terms):
                 for h in range(HALVES):
                     for mb in range(M_BLOCKS):
-                        turn(pages_b[c % 2], h, mb, mb == 0, False)
-            for cols in (slice(0, BANK), slice(BANK, T2)) if last else (slice(0, T2),):
-                nc.vector.scalar_tensor_tensor(
-                    out=boosted[:, cols], in0=pages_a[c % 2][:, cols], scalar=1.0, in1=vis_sb[c][:, cols], op0=ALU.add, op1=ALU.mult
-                )
+                        nc.tensor.matmul(
+                            sum_banks[c % 2][h][:, mb * P : (mb + 1) * P],
+                            lhsT=term[:, h * BANK + mb * P : h * BANK + (mb + 1) * P], rhs=ident[:], is_transpose=True,
+                            start=(i == 0 and mb == 0), stop=(i == len(terms) - 1 and mb == M_BLOCKS - 1),
+                        )
             for h in range(HALVES):
                 if quad == 0:
                     z_t[h] = ring.tile([P, M_BLOCKS * K_PASS], BF16, name=f"z_t{h}", tag=f"z_t{h}")
                 bank = sum_banks[c % 2][h]
-                for mb in range(M_BLOCKS):
-                    if last:
-                        turn(boosted, h, mb, False, mb == M_BLOCKS - 1)
-                    else:
-                        turn(boosted, h, mb, True, False)
-                        turn(pages_b[c % 2], h, mb, False, True)
                 copy = nc.vector.tensor_copy if last and h == 1 else nc.scalar.copy
                 copy(
                     out=z_t[h][:].rearrange("m (mb u t q e) -> m mb u t q e", mb=M_BLOCKS, u=2, t=TILES_PER_PASS, e=2)[:, :, :, quad, :, :],
@@ -271,7 +278,6 @@ def tile_list_alert_queue_ranker_kernel(
             nc.vector.tensor_copy(v_w[a][:], tab_w[a][:].bitcast(U32).indirect(offs_sb[:]))
         nc.tensor.transpose(banks[6][:, :P], gain_rows[:], ident[:])
         nc.scalar.copy(out=gain_sb[:], in_=banks[6][:, :TILES])
-        nc.scalar.activation(out=wg1_abs[:], in_=wg1_sb[:], func=ACT.Abs)
         stage_h1(0)
         stage_h2(1)
         stage_h1(1)
@@ -296,22 +302,27 @@ def tile_list_alert_queue_ranker_kernel(
         for c in range(3, 6):
             load_vis(c)
         place_a(0)
+        place_a(1)
 
         held_pairs = ((banks[4], banks[5]), (banks[0], banks[1]), (banks[2], banks[3]))
         for c in range(TILES):
             if c + 2 < TILES:
                 stage_h1(c + 2)
                 stage_h2(c + 2)
-            if c + 1 < TILES:
-                place_a(c + 1)
+            if c < TILES - 1:
+                scale_vis(c)
+            if c + 2 < TILES:
+                place_a(c + 2)
             if c == TILES - 1:
                 for n in range(N_TILES):
                     read_queue(held_pairs[n], n, 0, range(R_PASSES - 1))
             combine(c)
+            if c + 2 == TILES - 1:
+                scale_vis(c + 2)
+            if c + 2 < TILES:
+                place_b(c + 2)
             if c + 6 < TILES:
                 load_vis(c + 6)
-            if 1 <= c + 1 < TILES and c >= 1:
-                place_b(c + 1)
             if c % TILES_PER_PASS == TILES_PER_PASS - 1:
                 quantise_z(c // TILES_PER_PASS)
             if 4 <= c < 4 + R_PASSES:

@@ -31,7 +31,10 @@ HALVES = T2 // BANK
 M_BLOCKS = BANK // P
 N_TILES = N // P
 QUADS = 4
-HEAD_TILES = 2
+HEAD_TILES = 1
+PAGES = 2
+W1_GROUPS = ((0,), (1,), (2,), (3,), (4, 5))
+W3_CUT = 1024
 
 
 def tile_list_alert_queue_ranker_kernel(
@@ -47,8 +50,10 @@ def tile_list_alert_queue_ranker_kernel(
         banks = [psum.tile([P, BANK], F32, name=f"bank{i}") for i in range(8)]
         h1_banks = (banks[0], banks[4])
         h2_banks = (banks[1], banks[5])
-        sum_banks = ((banks[2], banks[3]), (banks[6], banks[7]))
         turn_banks = (banks[6], banks[7])
+
+        def sum_banks(c):
+            return (banks[2], banks[3]) if c % 2 == 0 and c < TILES - 2 else turn_banks
 
         offs_sb = keep.tile([P, S // 16], U16, name="offs_sb")
         offs2_sb = keep.tile([P, S // 16], U16, name="offs2_sb")
@@ -62,29 +67,24 @@ def tile_list_alert_queue_ranker_kernel(
         v_s = keep.tile([P, S], U8, name="v_s", align_bytes=64)
         v2_w = keep.tile([P, S], U32, name="v2_w", align_bytes=64)
         v2_s = keep.tile([P, S], U8, name="v2_s", align_bytes=64)
-        w2_first = keep.tile([P, 2 * P], U8, name="w2_first", align_bytes=64)
-        w2_rest = keep.tile([P, 2 * (H - P)], U8, name="w2_rest", align_bytes=64)
+        w2_w = keep.tile([P, 2 * H], U8, name="w2_w", align_bytes=64)
         w2_s = keep.tile([P, H], U8, name="w2_s", align_bytes=64)
         w4_w = keep.tile([P, R_PASSES * 2 * N], U8, name="w4_w", align_bytes=64)
         w4_s = keep.tile([P, R_PASSES * N], U8, name="w4_s", align_bytes=64)
-        w1_q = [keep.tile([P, K_PASSES * W1_COLS], U32, name=f"w1_q{k}", align_bytes=64) for k in range(W1_CHUNKS)]
-        w1_s = [keep.tile([P, K_PASSES * W1_COLS], U8, name=f"w1_s{k}", align_bytes=64) for k in range(W1_CHUNKS)]
-        w3_q = [keep.tile([P, N], U32, name=f"w3_q{b}", align_bytes=64) for b in range(R_PASSES)]
-        w3_s = [keep.tile([P, N], U8, name=f"w3_s{b}", align_bytes=64) for b in range(R_PASSES)]
-        z_q = [[keep.tile([P, BANK], U32, name=f"z_q{b}{h}", align_bytes=64) for h in range(HALVES)] for b in range(R_PASSES)]
-        z_s = [[keep.tile([P, BANK], U8, name=f"z_s{b}{h}", align_bytes=64) for h in range(HALVES)] for b in range(R_PASSES)]
+        follows = {7: "z_q0", 8: "w3_q0", 9: "w3_q1", 10: "z_q1"}
+
         wg1_sb = keep.tile([P, S], F32, name="wg1_sb")
         wg2_sb = keep.tile([P, S], F32, name="wg2_sb")
         gain_rows = keep.tile([P, P], F32, name="gain_rows")
         gain_sb = keep.tile([P, TILES], F32, name="gain_sb")
         ident = keep.tile([P, P], F32, name="ident")
-        pages_a = [keep.tile([P, T2], F32, name=f"page_a{i}") for i in range(2)]
-        pages_b = [keep.tile([P, T2], F32, name=f"page_b{i}") for i in range(2)]
+        pages_a = [keep.tile([P, T2], F32, name=f"page_a{i}") for i in range(PAGES)]
+        pages_b = [keep.tile([P, T2], F32, name=f"page_b{i}") for i in range(PAGES)]
 
-        def load_scales(engine, plane, scales):
+        def load_scales(plane, scales):
             passes = scales.shape[0]
             for q in range(QUADS):
-                engine.dma_start(
+                nc.sync.dma_start(
                     out=plane[32 * q : 32 * q + 4 * passes, :].bitcast(I32),
                     in_=scales[:, 4 * q : 4 * q + 4, :].bitcast(I32),
                 )
@@ -92,26 +92,16 @@ def tile_list_alert_queue_ranker_kernel(
         def table_words(words, a):
             return words[a].rearrange("p t i -> p (t i)").bitcast(I32)
 
+        def load_w2(lo, hi):
+            nc.sync.dma_start(out=w2_w[:, 2 * P * lo : 2 * P * hi].bitcast(I32), in_=w2_words[0][:, 2 * P * lo : 2 * P * hi].bitcast(I32))
+
+        make_identity(nc, ident[:])
         for plane in (tab2_s, w2_s, tab_s):
             nc.vector.memset(plane[:].bitcast(I32), 0)
-        nc.sync.dma_start(offs2_sb[:], offs2)
-        nc.sync.dma_start(out=w2_first[:].bitcast(I32), in_=w2_words[0][:, : 2 * P].bitcast(I32))
-        nc.sync.dma_start(offs4_sb[:], offs4)
-        nc.sync.dma_start(offs_sb[:], offs)
-        nc.sync.dma_start(offs3_sb[:], offs3)
-        nc.sync.dma_start(out=tab2_w[:], in_=table_words(tab2_words, 0))
-        load_scales(nc.sync, tab2_s, tab2_scales)
-        load_scales(nc.sync, w2_s, w2_scales)
-        load_scales(nc.sync, tab_s, tab_scales)
-        nc.sync.dma_start(out=wg2_sb[:], in_=wg2)
         for page in pages_b:
             nc.vector.memset(page[:], 0.0)
-        nc.gpsimd.memset(gain_rows[:], 0.0)
-        nc.gpsimd.dma_start(out=gain_rows[:TILES, :], in_=gain.rearrange("(c p) -> c p", p=P))
-        make_identity(nc, ident[:])
-        for page in pages_a:
-            nc.gpsimd.memset(page[:], 0.0)
-        nc.gpsimd.memset(w4_s[:].bitcast(I32), 0)
+        nc.vector.memset(w4_s[:].bitcast(I32), 0)
+        nc.vector.memset(gain_rows[:], 0.0)
 
         w1_raw = {}
 
@@ -132,29 +122,74 @@ def tile_list_alert_queue_ranker_kernel(
             nc.sync.dma_start(out=raw[:], in_=w3[b * K_PASS : (b + 1) * K_PASS, :].rearrange("(p j) n -> p (j n)", j=PACK))
             w3_raw[b] = raw
 
-        def quantise_weight(raw, codes, scales):
-            width = raw.shape[1]
-            grouped = ring.tile([P, width], BF16, name="w_bf", tag="w_bf", align_bytes=64)
-            nc.scalar.copy(
-                out=grouped[:].rearrange("p (g i j) -> p g j i", i=4, j=PACK),
-                in_=raw[:].rearrange("p (j g i) -> p g j i", i=4, j=PACK),
-            )
-            nc.vector.quantize_mx(out=codes[:].bitcast(FP8X4), scales=scales[:], in_=grouped[:])
+        def round_weight(raws, tag, bufs):
+            width = raws[0].shape[1]
+            grouped = ring.tile([P, len(raws) * width], BF16, name=tag, tag=tag, bufs=bufs, align_bytes=64)
+            for n, raw in enumerate(raws):
+                dst = grouped[:, n * width : (n + 1) * width].rearrange("p (g i j) -> p g j i", i=4, j=PACK)
+                src = raw[:].rearrange("p (j g i) -> p g j i", i=4, j=PACK)
+                half = src.shape[1] // 2
+                for part in (slice(0, half), slice(half, 2 * half)):
+                    nc.scalar.copy(out=dst[:, part], in_=src[:, part])
+            return grouped
+
+        def quantise(name, grouped):
+            words = grouped.shape[1] // PACK
+            codes = ring.tile([P, words], U32, name=name, tag=name, bufs=1, align_bytes=64)
+            scales = ring.tile([P, words], U8, name=name + "s", tag=name + "s", bufs=1, align_bytes=64)
+            nc.vector.quantize_mx(out=codes[:].bitcast(FP8X4), scales=scales[:], in_=grouped)
+            return codes, scales
+
+        w1_bf = {}
+        w1_q = {}
+
+        def round_w1(g):
+            w1_bf[g] = round_weight([w1_raw[k] for k in W1_GROUPS[g]], "w1_bf", 2)
+
+        def quantise_w1(g):
+            group = W1_GROUPS[g]
+            span = K_PASSES * W1_COLS
+            planes = quantise(f"w1_q{g}", w1_bf[g][:])
+            for n, k in enumerate(group):
+                w1_q[k] = [plane[:, n * span : (n + 1) * span] for plane in planes]
 
         vis_sb = {}
 
         def load_vis(c):
-            tile = ring.tile([P, T2], F32, name="vis_sb", tag="vis_sb", bufs=6)
+            if c + 2 in follows:
+                tile = ring.tile([P, T2], F32, name="vis_own", tag=follows[c + 2], bufs=1, align_bytes=64)
+            else:
+                tile = ring.tile([P, T2], F32, name="vis_sb", tag="vis_sb", bufs=3)
             nc.sync.dma_start(out=tile[:], in_=vis[c * P : (c + 1) * P, :])
             vis_sb[c] = tile
 
-        load_w1(0)
+        nc.sync.dma_start(offs2_sb[:], offs2)
+        load_w2(0, 1)
+        nc.sync.dma_start(offs_sb[:], offs)
+        nc.sync.dma_start(out=tab2_w[:], in_=table_words(tab2_words, 0))
+        load_scales(tab2_s, tab2_scales)
+        load_scales(w2_s, w2_scales)
+        load_scales(tab_s, tab_scales)
+        nc.gpsimd.dma_start(out=gain_rows[:TILES, :], in_=gain.rearrange("(c p) -> c p", p=P))
+        nc.sync.dma_start(out=wg2_sb[:], in_=wg2)
+        nc.sync.dma_start(offs4_sb[:], offs4)
         nc.sync.dma_start(out=tab_w[0][:], in_=table_words(tab_words, 0))
+        load_w1(0)
+        load_w2(1, 2)
         nc.sync.dma_start(out=tab_w[1][:], in_=table_words(tab_words, 1))
-        nc.sync.dma_start(out=w2_rest[:].bitcast(I32), in_=w2_words[0][:, 2 * P :].bitcast(I32))
         nc.sync.dma_start(out=wg1_sb[:], in_=wg1)
-        for k in range(1, 3):
-            load_w1(k)
+        nc.sync.dma_start(offs3_sb[:], offs3)
+        load_w2(2, TILES)
+        load_vis(0)
+        load_w1(1)
+        load_w1(2)
+
+        boost = {}
+
+        def scratch(c):
+            if c not in boost:
+                boost[c] = ring.tile([P, T2], F32, name="boost", tag="boost", bufs=3)
+            return boost[c]
 
         h1_sb = {}
         h2_sb = {}
@@ -163,102 +198,126 @@ def tile_list_alert_queue_ranker_kernel(
             bank = h1_banks[c % 2]
             k, col = divmod(c * P, W1_COLS)
             for a in range(K_PASSES):
-                cols = slice(a * W1_COLS + col, a * W1_COLS + col + P)
+                lo = a * W1_COLS + col
                 nc.tensor.matmul_mx(
-                    out=bank[:], lhsT=w1_q[k][:, cols].bitcast(FP8X4), lhsT_scale=w1_s[k][:, cols],
+                    out=bank[:], lhsT=w1_q[k][0][:, lo : lo + P].bitcast(FP8X4), lhsT_scale=w1_q[k][1][:, lo : lo + P],
                     rhs=v_w[a][:].bitcast(FP8X4), rhs_scale=v_s[4 * a :, :],
                     start=(a == 0), stop=(a == K_PASSES - 1),
                 )
             tile = ring.tile([P, S], F32, name="h1_sb", tag="h1_sb", bufs=3)
-            nc.scalar.activation(out=tile[:], in_=bank[:], func=ACT.Tanh)
-            nc.gpsimd.tensor_tensor(tile[:], tile[:], wg1_sb[:], ALU.mult)
-            nc.scalar.activation(out=tile[:], in_=tile[:], func=ACT.Abs, scale=gain_sb[:, c : c + 1])
+            signed = tile
+            if c in follows:
+                signed = ring.tile([P, S], F32, name="signed", tag=follows[c] + "s", bufs=1, align_bytes=64)
+            raw = scratch(c - 1)[:, :S] if c > 0 else tile[:]
+            nc.scalar.activation(out=raw, in_=bank[:], func=ACT.Tanh)
+            nc.gpsimd.tensor_tensor(signed[:], raw, wg1_sb[:], ALU.mult)
+            nc.scalar.activation(out=tile[:], in_=signed[:], func=ACT.Abs, scale=gain_sb[:, c : c + 1])
             h1_sb[c] = tile
 
         def stage_h2(c):
             bank = h2_banks[c % 2]
-            words = w2_first[:] if c == 0 else w2_rest[:, 2 * P * (c - 1) : 2 * P * c]
+            words = w2_w[:, 2 * P * c : 2 * P * (c + 1)]
             nc.tensor.matmul_mx(
                 out=bank[:], lhsT=words.bitcast(FP4X4), lhsT_scale=w2_s[:, c * P : (c + 1) * P],
                 rhs=v2_w[:].bitcast(FP8X4), rhs_scale=v2_s[:], start=True, stop=True,
             )
             tile = ring.tile([P, S], F32, name="h2_sb", tag="h2_sb", bufs=3)
-            nc.scalar.copy(out=tile[:], in_=bank[:])
             if c >= HEAD_TILES:
-                nc.gpsimd.tensor_tensor(tile[:], tile[:], wg2_sb[:], ALU.mult)
+                raw = scratch(c - 1)[:, S:]
+                nc.scalar.copy(out=raw, in_=bank[:])
+                nc.gpsimd.tensor_tensor(tile[:], raw, wg2_sb[:], ALU.mult)
+            else:
+                nc.scalar.copy(out=tile[:], in_=bank[:])
             h2_sb[c] = tile
 
         def place_a(c):
-            nc.vector.tensor_copy(pages_a[c % 2][:].indirect(offs3_sb[:]), h1_sb[c][:])
+            nc.vector.tensor_copy(pages_a[c % PAGES][:].indirect(offs3_sb[:]), h1_sb[c][:])
 
         def place_b(c):
             if c >= HEAD_TILES:
-                nc.vector.tensor_copy(pages_b[c % 2][:].indirect(offs4_sb[:]), h2_sb[c][:])
+                nc.vector.tensor_copy(pages_b[c % PAGES][:].indirect(offs4_sb[:]), h2_sb[c][:])
             else:
-                nc.vector.tensor_tensor(pages_b[c % 2][:].indirect(offs4_sb[:]), h2_sb[c][:], wg2_sb[:], ALU.mult)
+                nc.vector.tensor_tensor(pages_b[c % PAGES][:].indirect(offs4_sb[:]), h2_sb[c][:], wg2_sb[:], ALU.mult)
 
         z_t = {}
 
-        boost = {}
+        def add_turned(c, term, h, start, stop):
+            for mb in range(M_BLOCKS):
+                nc.tensor.matmul(
+                    sum_banks(c)[h][:, mb * P : (mb + 1) * P],
+                    lhsT=term[:, h * BANK + mb * P : h * BANK + (mb + 1) * P], rhs=ident[:], is_transpose=True,
+                    start=(start and mb == 0), stop=(stop and mb == M_BLOCKS - 1),
+                )
 
         def scale_vis(c):
-            tile = ring.tile([P, T2], F32, name="boost", tag="boost")
-            if c == TILES - 1:
-                nc.vector.scalar_tensor_tensor(
-                    out=tile[:], in0=pages_a[c % 2][:], scalar=1.0, in1=vis_sb[c][:], op0=ALU.add, op1=ALU.mult
-                )
-            else:
-                for h in range(HALVES):
-                    cols = slice(h * BANK, (h + 1) * BANK)
-                    nc.gpsimd.tensor_tensor(tile[:, cols], pages_a[c % 2][:, cols], vis_sb[c][:, cols], ALU.mult)
-            boost[c] = tile
+            nc.gpsimd.tensor_tensor(scratch(c)[:], pages_a[c % PAGES][:], vis_sb[c][:], ALU.mult)
 
         def combine(c):
             b, quad = divmod(c, TILES_PER_PASS)
             last = c == TILES - 1
-            terms = (boost[c], pages_b[c % 2]) if last else (vis_sb[c], boost[c], pages_b[c % 2])
-            for i, term in enumerate(terms):
+            if last:
                 for h in range(HALVES):
-                    for mb in range(M_BLOCKS):
-                        nc.tensor.matmul(
-                            sum_banks[c % 2][h][:, mb * P : (mb + 1) * P],
-                            lhsT=term[:, h * BANK + mb * P : h * BANK + (mb + 1) * P], rhs=ident[:], is_transpose=True,
-                            start=(i == 0 and mb == 0), stop=(i == len(terms) - 1 and mb == M_BLOCKS - 1),
-                        )
+                    add_turned(c, pages_b[c % PAGES], h, True, False)
+                    cols = slice(h * BANK, (h + 1) * BANK)
+                    nc.vector.scalar_tensor_tensor(
+                        out=boost[c - 1][:, cols], in0=pages_a[c % PAGES][:, cols], scalar=1.0, in1=vis_sb[c][:, cols],
+                        op0=ALU.add, op1=ALU.mult,
+                    )
+                    add_turned(c, boost[c - 1], h, False, True)
+            else:
+                for i, term in enumerate((vis_sb[c], boost[c], pages_b[c % PAGES])):
+                    for h in range(HALVES):
+                        add_turned(c, term, h, i == 0, i == 2)
             for h in range(HALVES):
                 if quad == 0:
                     z_t[h] = ring.tile([P, M_BLOCKS * K_PASS], BF16, name=f"z_t{h}", tag=f"z_t{h}")
-                bank = sum_banks[c % 2][h]
+                bank = sum_banks(c)[h]
                 copy = nc.vector.tensor_copy if last and h == 1 else nc.scalar.copy
                 copy(
                     out=z_t[h][:].rearrange("m (mb u t q e) -> m mb u t q e", mb=M_BLOCKS, u=2, t=TILES_PER_PASS, e=2)[:, :, :, quad, :, :],
                     in_=bank[:].rearrange("m (mb q u e) -> m mb u q e", mb=M_BLOCKS, u=2, e=2),
                 )
 
-        def quantise_z(b):
+        z_bf = {}
+        z_q = {}
+        w3_q = []
+
+        def turn_z(b):
+            last = b == R_PASSES - 1
+            grouped = ring.tile([P, T2 * PACK], BF16, name="z_bf", tag="z_bf", bufs=1, align_bytes=64)
+            pairs = grouped[:].bitcast(F32).rearrange("p (m u) -> p m u", u=2)
             for h in range(HALVES):
                 words = z_t[h][:].bitcast(F32).rearrange("m (mb u p) -> m mb u p", mb=M_BLOCKS, u=2)
-                grouped = ring.tile([P, BANK * PACK], BF16, name="z_bf", tag="z_bf", align_bytes=64)
-                pairs = grouped[:].bitcast(F32).rearrange("p (m u) -> p m u", u=2)
                 for i, bank in enumerate(turn_banks):
                     for u in range(2):
                         for j in range(2):
                             nc.tensor.transpose(bank[:, (2 * u + j) * P : (2 * u + j + 1) * P], words[:, 2 * i + j, u, :], ident[:])
-                    copy = nc.vector.tensor_copy if b == R_PASSES - 1 and i == 1 else nc.scalar.copy
-                    copy(out=pairs[:, 2 * i * P : 2 * (i + 1) * P, :], in_=bank[:].rearrange("p (u m) -> p m u", u=2))
-                nc.vector.quantize_mx(out=z_q[b][h][:].bitcast(FP8X4), scales=z_s[b][h][:], in_=grouped[:])
+                    copy = nc.vector.tensor_copy if last and i == 1 else nc.scalar.copy
+                    m0 = h * BANK + 2 * i * P
+                    copy(out=pairs[:, m0 : m0 + 2 * P, :], in_=bank[:].rearrange("p (u m) -> p m u", u=2))
+                if last:
+                    lo, hi = h * BANK, (h + 1) * BANK
+                    z_q[b, h] = [plane[:] for plane in quantise(f"z_q{b}{h}", grouped[:, PACK * lo : PACK * hi])]
+            z_bf[b] = grouped
+
+        def quantise_z(b):
+            planes = quantise(f"z_q{b}", z_bf[b][:])
+            for h in range(HALVES):
+                z_q[b, h] = [plane[:, h * BANK : (h + 1) * BANK] for plane in planes]
 
         def read_queue(pair, n, h, passes):
             for b in passes:
                 col = b * N + n * P
                 nc.tensor.matmul_mx(
                     out=pair[1][:], lhsT=w4_w[:, 2 * col : 2 * (col + P)].bitcast(FP4X4), lhsT_scale=w4_s[:, col : col + P],
-                    rhs=z_q[b][h][:].bitcast(FP8X4), rhs_scale=z_s[b][h][:], start=(b == 0), stop=(b == R_PASSES - 1),
+                    rhs=z_q[b, h][0].bitcast(FP8X4), rhs_scale=z_q[b, h][1], start=(b == 0), stop=(b == R_PASSES - 1),
                 )
             for b in passes:
+                col = b * N + n * P
                 nc.tensor.matmul_mx(
-                    out=pair[0][:], lhsT=w3_q[b][:, n * P : (n + 1) * P].bitcast(FP8X4), lhsT_scale=w3_s[b][:, n * P : (n + 1) * P],
-                    rhs=z_q[b][h][:].bitcast(FP8X4), rhs_scale=z_s[b][h][:], start=(b == 0), stop=(b == R_PASSES - 1),
+                    out=pair[0][:], lhsT=w3_q[col // W3_CUT][0][:, col % W3_CUT : col % W3_CUT + P].bitcast(FP8X4),
+                    lhsT_scale=w3_q[col // W3_CUT][1][:, col % W3_CUT : col % W3_CUT + P],
+                    rhs=z_q[b, h][0].bitcast(FP8X4), rhs_scale=z_q[b, h][1], start=(b == 0), stop=(b == R_PASSES - 1),
                 )
 
         def finish(pair, n, h):
@@ -271,36 +330,38 @@ def tile_list_alert_queue_ranker_kernel(
         nc.vector.tensor_copy(v2_s[:], tab2_s[:].indirect(offs2_sb[:]))
         nc.vector.tensor_copy(v2_w[:], tab2_w[:].bitcast(U32).indirect(offs2_sb[:]))
         stage_h2(0)
+        for page in pages_a:
+            nc.vector.memset(page[:], 0.0)
         nc.vector.tensor_copy(v_s[:], tab_s[:].indirect(offs_sb[:]))
         place_b(0)
-        quantise_weight(w1_raw[0], w1_q[0], w1_s[0])
+        round_w1(0)
+        quantise_w1(0)
         for a in range(K_PASSES):
             nc.vector.tensor_copy(v_w[a][:], tab_w[a][:].bitcast(U32).indirect(offs_sb[:]))
         nc.tensor.transpose(banks[6][:, :P], gain_rows[:], ident[:])
         nc.scalar.copy(out=gain_sb[:], in_=banks[6][:, :TILES])
-        stage_h1(0)
         stage_h2(1)
+        stage_h1(0)
+        round_w1(1)
+        quantise_w1(1)
         stage_h1(1)
         place_b(1)
-        for k in range(1, W1_CHUNKS):
-            quantise_weight(w1_raw[k], w1_q[k], w1_s[k])
-            if k + 2 < W1_CHUNKS:
-                load_w1(k + 2)
-        for c in range(3):
-            load_vis(c)
-        for b in range(R_PASSES):
-            load_w3(b)
-        nc.sync.dma_start(
-            out=w4_w[:].bitcast(I32).rearrange("p (a n) -> p a n", a=R_PASSES),
-            in_=w4_words.bitcast(I32).rearrange("a p n -> p a n"),
-        )
-        for q in range(QUADS):
+        load_vis(1)
+        load_w1(3)
+
+        def load_second_stage():
+            for b in range(R_PASSES):
+                load_w3(b)
             nc.sync.dma_start(
-                out=w4_s[32 * q : 32 * q + 4, :].bitcast(I32).rearrange("r (a n) -> r a n", a=R_PASSES),
-                in_=w4_scales[:, 4 * q : 4 * q + 4, :].bitcast(I32).rearrange("a r n -> r a n"),
+                out=w4_w[:].bitcast(I32).rearrange("p (a n) -> p a n", a=R_PASSES),
+                in_=w4_words.bitcast(I32).rearrange("a p n -> p a n"),
             )
-        for c in range(3, 6):
-            load_vis(c)
+            for q in range(QUADS):
+                nc.sync.dma_start(
+                    out=w4_s[32 * q : 32 * q + 4, :].bitcast(I32).rearrange("r (a n) -> r a n", a=R_PASSES),
+                    in_=w4_scales[:, 4 * q : 4 * q + 4, :].bitcast(I32).rearrange("a r n -> r a n"),
+                )
+
         place_a(0)
         place_a(1)
 
@@ -313,20 +374,41 @@ def tile_list_alert_queue_ranker_kernel(
                 scale_vis(c)
             if c + 2 < TILES:
                 place_a(c + 2)
+            if c == 2:
+                quantise_w1(3)
+            if c == 3:
+                quantise_w1(4)
+            if c == 5:
+                quantise_z(0)
+                w3_bf = round_weight([w3_raw[b] for b in range(R_PASSES)], "w3_bf", 1)
+            if c == 6:
+                w3_q.append(quantise("w3_q0", w3_bf[:, : PACK * W3_CUT]))
+            if c == 7:
+                w3_q.append(quantise("w3_q1", w3_bf[:, PACK * W3_CUT :]))
+            if c == 8:
+                quantise_z(1)
             if c == TILES - 1:
                 for n in range(N_TILES):
                     read_queue(held_pairs[n], n, 0, range(R_PASSES - 1))
             combine(c)
-            if c + 2 == TILES - 1:
-                scale_vis(c + 2)
             if c + 2 < TILES:
                 place_b(c + 2)
-            if c + 6 < TILES:
-                load_vis(c + 6)
+            if c == 0:
+                round_w1(2)
+                quantise_w1(2)
+                load_w1(4)
+                load_vis(2)
+                round_w1(3)
+                load_w1(5)
+                load_vis(3)
+            if c == 1:
+                round_w1(4)
+            if c + 4 < TILES:
+                load_vis(c + 4)
+            if c == 1:
+                load_second_stage()
             if c % TILES_PER_PASS == TILES_PER_PASS - 1:
-                quantise_z(c // TILES_PER_PASS)
-            if 4 <= c < 4 + R_PASSES:
-                quantise_weight(w3_raw[c - 4], w3_q[c - 4], w3_s[c - 4])
+                turn_z(c // TILES_PER_PASS)
 
         for n in range(N_TILES):
             read_queue(held_pairs[n], n, 0, [R_PASSES - 1])

@@ -19,22 +19,24 @@ ACT = mybir.ActivationFunctionType
 
 P = 128
 PACK = 4
-K_PASS = P * PACK
+PASS = P * PACK
 BANK = 512
+QUADS = 4
 TILES = H // P
-R_PASSES = H // K_PASS
-TILES_PER_PASS = K_PASS // P
-K_PASSES = K // K_PASS
-W1_COLS = 256
-W1_CHUNKS = H // W1_COLS
+TILES_PER_PASS = PASS // P
+K_PASSES = K // PASS
+R_PASSES = H // PASS
 HALVES = T2 // BANK
 M_BLOCKS = BANK // P
 N_TILES = N // P
-QUADS = 4
-HEAD_TILES = 1
-PAGES = 2
-W1_GROUPS = ((0,), (1,), (2,), (3,), (4, 5))
+W1_COLS = 2 * P
+W1_CHUNKS = H // W1_COLS
 W3_CUT = 1024
+AHEAD = 2
+PAGES = 2
+STAGED = AHEAD + 1
+RAW_BUFS = 3
+VIS_AHEAD = 4
 
 
 def tile_list_alert_queue_ranker_kernel(
@@ -50,10 +52,13 @@ def tile_list_alert_queue_ranker_kernel(
         banks = [psum.tile([P, BANK], F32, name=f"bank{i}") for i in range(8)]
         h1_banks = (banks[0], banks[4])
         h2_banks = (banks[1], banks[5])
+        even_banks = (banks[2], banks[3])
         turn_banks = (banks[6], banks[7])
+        held_pairs = ((banks[4], banks[5]), (banks[0], banks[1]), even_banks)
+        late_pairs = (turn_banks, held_pairs[0], held_pairs[1])
 
         def sum_banks(c):
-            return (banks[2], banks[3]) if c % 2 == 0 and c < TILES - 2 else turn_banks
+            return even_banks if c % 2 == 0 and c < TILES - 2 else turn_banks
 
         offs_sb = keep.tile([P, S // 16], U16, name="offs_sb")
         offs2_sb = keep.tile([P, S // 16], U16, name="offs2_sb")
@@ -71,17 +76,22 @@ def tile_list_alert_queue_ranker_kernel(
         w2_s = keep.tile([P, H], U8, name="w2_s", align_bytes=64)
         w4_w = keep.tile([P, R_PASSES * 2 * N], U8, name="w4_w", align_bytes=64)
         w4_s = keep.tile([P, R_PASSES * N], U8, name="w4_s", align_bytes=64)
-        follows = {7: "z_q0", 8: "w3_q0", 9: "w3_q1", 10: "z_q1"}
-
         wg1_sb = keep.tile([P, S], F32, name="wg1_sb")
+        wg1_abs = keep.tile([P, S], F32, name="wg1_abs")
         wg2_sb = keep.tile([P, S], F32, name="wg2_sb")
         gain_rows = keep.tile([P, P], F32, name="gain_rows")
         gain_sb = keep.tile([P, TILES], F32, name="gain_sb")
         ident = keep.tile([P, P], F32, name="ident")
         pages_a = [keep.tile([P, T2], F32, name=f"page_a{i}") for i in range(PAGES)]
         pages_b = [keep.tile([P, T2], F32, name=f"page_b{i}") for i in range(PAGES)]
+        boosted = [keep.tile([P, T2], F32, name=f"boosted{i}") for i in range(PAGES)]
 
-        def load_scales(plane, scales):
+        w1_raw, w3_raw, vis_sb, h1_sb, h2_sb = {}, {}, {}, {}, {}
+        w1_q, z_t, z_q = {}, {}, {}
+        w3_q = []
+
+
+        def load_plane(plane, scales):
             passes = scales.shape[0]
             for q in range(QUADS):
                 nc.sync.dma_start(
@@ -89,200 +99,136 @@ def tile_list_alert_queue_ranker_kernel(
                     in_=scales[:, 4 * q : 4 * q + 4, :].bitcast(I32),
                 )
 
-        def table_words(words, a):
-            return words[a].rearrange("p t i -> p (t i)").bitcast(I32)
+        def load_table(tile, words, a):
+            nc.sync.dma_start(out=tile[:], in_=words[a].rearrange("p t i -> p (t i)").bitcast(I32))
 
-        def load_w2(lo, hi):
-            nc.sync.dma_start(out=w2_w[:, 2 * P * lo : 2 * P * hi].bitcast(I32), in_=w2_words[0][:, 2 * P * lo : 2 * P * hi].bitcast(I32))
-
-        make_identity(nc, ident[:])
-        for plane in (tab2_s, w2_s, tab_s):
-            nc.vector.memset(plane[:].bitcast(I32), 0)
-        for page in pages_b:
-            nc.vector.memset(page[:], 0.0)
-        nc.vector.memset(w4_s[:].bitcast(I32), 0)
-        nc.vector.memset(gain_rows[:], 0.0)
-
-        w1_raw = {}
+        def load_w2(first, end):
+            cols = slice(2 * P * first, 2 * P * end)
+            nc.sync.dma_start(out=w2_w[:, cols].bitcast(I32), in_=w2_words[0][:, cols].bitcast(I32))
 
         def load_w1(k):
-            raw = ring.tile([P, PACK * K_PASSES * W1_COLS], F32, name="w_raw", tag="w_raw", bufs=3)
+            raw = ring.tile([P, PACK * K_PASSES * W1_COLS], F32, name="w_raw", tag="w_raw", bufs=RAW_BUFS)
             view = raw[:].rearrange("p (j a c) -> p j a c", j=PACK, a=K_PASSES)
             for a in range(K_PASSES):
-                nc.sync.dma_start(
-                    out=view[:, :, a, :],
-                    in_=w1[a * K_PASS : (a + 1) * K_PASS, k * W1_COLS : (k + 1) * W1_COLS].rearrange("(p j) c -> p j c", j=PACK),
-                )
+                rows = w1[a * PASS : (a + 1) * PASS, k * W1_COLS : (k + 1) * W1_COLS]
+                nc.sync.dma_start(out=view[:, :, a, :], in_=rows.rearrange("(p j) c -> p j c", j=PACK))
             w1_raw[k] = raw
 
-        w3_raw = {}
+        def load_vis(c):
+            vis_sb[c] = ring.tile([P, T2], F32, name="vis_sb", tag="vis_sb", bufs=VIS_AHEAD + 1)
+            nc.sync.dma_start(out=vis_sb[c][:], in_=vis[c * P : (c + 1) * P, :])
 
-        def load_w3(b):
-            raw = ring.tile([P, PACK * N], F32, name="w_raw", tag="w_raw", bufs=3)
-            nc.sync.dma_start(out=raw[:], in_=w3[b * K_PASS : (b + 1) * K_PASS, :].rearrange("(p j) n -> p (j n)", j=PACK))
-            w3_raw[b] = raw
+        def load_second_stage():
+            for b in range(R_PASSES):
+                w3_raw[b] = ring.tile([P, PACK * N], F32, name="w_raw", tag="w_raw", bufs=RAW_BUFS)
+                rows = w3[b * PASS : (b + 1) * PASS, :]
+                nc.sync.dma_start(out=w3_raw[b][:], in_=rows.rearrange("(p j) n -> p (j n)", j=PACK))
+            nc.sync.dma_start(
+                out=w4_w[:].bitcast(I32).rearrange("p (b n) -> p b n", b=R_PASSES),
+                in_=w4_words.bitcast(I32).rearrange("b p n -> p b n"),
+            )
+            for q in range(QUADS):
+                nc.sync.dma_start(
+                    out=w4_s[32 * q : 32 * q + 4, :].bitcast(I32).rearrange("r (b n) -> r b n", b=R_PASSES),
+                    in_=w4_scales[:, 4 * q : 4 * q + 4, :].bitcast(I32).rearrange("b r n -> r b n"),
+                )
 
-        def round_weight(raws, tag, bufs):
-            width = raws[0].shape[1]
-            grouped = ring.tile([P, len(raws) * width], BF16, name=tag, tag=tag, bufs=bufs, align_bytes=64)
-            for n, raw in enumerate(raws):
-                dst = grouped[:, n * width : (n + 1) * width].rearrange("p (g i j) -> p g j i", i=4, j=PACK)
-                src = raw[:].rearrange("p (j g i) -> p g j i", i=4, j=PACK)
-                half = src.shape[1] // 2
-                for part in (slice(0, half), slice(half, 2 * half)):
-                    nc.scalar.copy(out=dst[:, part], in_=src[:, part])
-            return grouped
+
+        def round_weight(grouped, raw):
+            dst = grouped.rearrange("p (g i j) -> p g j i", i=4, j=PACK)
+            src = raw[:].rearrange("p (j g i) -> p g j i", i=4, j=PACK)
+            half = src.shape[1] // 2
+            for part in (slice(0, half), slice(half, 2 * half)):
+                nc.scalar.copy(out=dst[:, part], in_=src[:, part])
 
         def quantise(name, grouped):
             words = grouped.shape[1] // PACK
-            codes = ring.tile([P, words], U32, name=name, tag=name, bufs=1, align_bytes=64)
-            scales = ring.tile([P, words], U8, name=name + "s", tag=name + "s", bufs=1, align_bytes=64)
-            nc.vector.quantize_mx(out=codes[:].bitcast(FP8X4), scales=scales[:], in_=grouped)
-            return codes, scales
+            codes = keep.tile([P, words], U32, name=name, align_bytes=64)
+            plane = keep.tile([P, words], U8, name=name + "s", align_bytes=64)
+            nc.vector.quantize_mx(out=codes[:].bitcast(FP8X4), scales=plane[:], in_=grouped)
+            return codes, plane
 
-        w1_bf = {}
-        w1_q = {}
+        def prepare_w1(k):
+            grouped = ring.tile([P, PACK * K_PASSES * W1_COLS], BF16, name="w1_bf", tag="w1_bf", align_bytes=64)
+            round_weight(grouped[:], w1_raw[k])
+            w1_q[k] = quantise(f"w1_q{k}", grouped[:])
 
-        def round_w1(g):
-            w1_bf[g] = round_weight([w1_raw[k] for k in W1_GROUPS[g]], "w1_bf", 2)
+        def prepare_w3():
+            grouped = keep.tile([P, R_PASSES * PACK * N], BF16, name="w3_bf", align_bytes=64)
+            for b in range(R_PASSES):
+                round_weight(grouped[:, b * PACK * N : (b + 1) * PACK * N], w3_raw[b])
+            w3_q.append(quantise("w3_q0", grouped[:, : PACK * W3_CUT]))
+            w3_q.append(quantise("w3_q1", grouped[:, PACK * W3_CUT :]))
 
-        def quantise_w1(g):
-            group = W1_GROUPS[g]
-            span = K_PASSES * W1_COLS
-            planes = quantise(f"w1_q{g}", w1_bf[g][:])
-            for n, k in enumerate(group):
-                w1_q[k] = [plane[:, n * span : (n + 1) * span] for plane in planes]
-
-        vis_sb = {}
-
-        def load_vis(c):
-            if c + 2 in follows:
-                tile = ring.tile([P, T2], F32, name="vis_own", tag=follows[c + 2], bufs=1, align_bytes=64)
-            else:
-                tile = ring.tile([P, T2], F32, name="vis_sb", tag="vis_sb", bufs=3)
-            nc.sync.dma_start(out=tile[:], in_=vis[c * P : (c + 1) * P, :])
-            vis_sb[c] = tile
-
-        nc.sync.dma_start(offs2_sb[:], offs2)
-        load_w2(0, 1)
-        nc.sync.dma_start(offs_sb[:], offs)
-        nc.sync.dma_start(out=tab2_w[:], in_=table_words(tab2_words, 0))
-        load_scales(tab2_s, tab2_scales)
-        load_scales(w2_s, w2_scales)
-        load_scales(tab_s, tab_scales)
-        nc.gpsimd.dma_start(out=gain_rows[:TILES, :], in_=gain.rearrange("(c p) -> c p", p=P))
-        nc.sync.dma_start(out=wg2_sb[:], in_=wg2)
-        nc.sync.dma_start(offs4_sb[:], offs4)
-        nc.sync.dma_start(out=tab_w[0][:], in_=table_words(tab_words, 0))
-        load_w1(0)
-        load_w2(1, 2)
-        nc.sync.dma_start(out=tab_w[1][:], in_=table_words(tab_words, 1))
-        nc.sync.dma_start(out=wg1_sb[:], in_=wg1)
-        nc.sync.dma_start(offs3_sb[:], offs3)
-        load_w2(2, TILES)
-        load_vis(0)
-        load_w1(1)
-        load_w1(2)
-
-        boost = {}
-
-        def scratch(c):
-            if c not in boost:
-                boost[c] = ring.tile([P, T2], F32, name="boost", tag="boost", bufs=3)
-            return boost[c]
-
-        h1_sb = {}
-        h2_sb = {}
 
         def stage_h1(c):
             bank = h1_banks[c % 2]
             k, col = divmod(c * P, W1_COLS)
+            codes, plane = w1_q[k]
             for a in range(K_PASSES):
-                lo = a * W1_COLS + col
+                cols = slice(a * W1_COLS + col, a * W1_COLS + col + P)
                 nc.tensor.matmul_mx(
-                    out=bank[:], lhsT=w1_q[k][0][:, lo : lo + P].bitcast(FP8X4), lhsT_scale=w1_q[k][1][:, lo : lo + P],
+                    out=bank[:], lhsT=codes[:, cols].bitcast(FP8X4), lhsT_scale=plane[:, cols],
                     rhs=v_w[a][:].bitcast(FP8X4), rhs_scale=v_s[4 * a :, :],
                     start=(a == 0), stop=(a == K_PASSES - 1),
                 )
-            tile = ring.tile([P, S], F32, name="h1_sb", tag="h1_sb", bufs=3)
-            signed = tile
-            if c in follows:
-                signed = ring.tile([P, S], F32, name="signed", tag=follows[c] + "s", bufs=1, align_bytes=64)
-            raw = scratch(c - 1)[:, :S] if c > 0 else tile[:]
-            nc.scalar.activation(out=raw, in_=bank[:], func=ACT.Tanh)
-            nc.gpsimd.tensor_tensor(signed[:], raw, wg1_sb[:], ALU.mult)
-            nc.scalar.activation(out=tile[:], in_=signed[:], func=ACT.Abs, scale=gain_sb[:, c : c + 1])
-            h1_sb[c] = tile
+            h1_sb[c] = ring.tile([P, S], F32, name="h1_sb", tag="h1_sb", bufs=STAGED)
+            nc.scalar.activation(out=h1_sb[c][:], in_=bank[:], func=ACT.Tanh)
+            nc.scalar.activation(out=h1_sb[c][:], in_=h1_sb[c][:], func=ACT.Abs, scale=gain_sb[:, c : c + 1])
 
         def stage_h2(c):
             bank = h2_banks[c % 2]
-            words = w2_w[:, 2 * P * c : 2 * P * (c + 1)]
             nc.tensor.matmul_mx(
-                out=bank[:], lhsT=words.bitcast(FP4X4), lhsT_scale=w2_s[:, c * P : (c + 1) * P],
+                out=bank[:], lhsT=w2_w[:, 2 * P * c : 2 * P * (c + 1)].bitcast(FP4X4), lhsT_scale=w2_s[:, c * P : (c + 1) * P],
                 rhs=v2_w[:].bitcast(FP8X4), rhs_scale=v2_s[:], start=True, stop=True,
             )
-            tile = ring.tile([P, S], F32, name="h2_sb", tag="h2_sb", bufs=3)
-            if c >= HEAD_TILES:
-                raw = scratch(c - 1)[:, S:]
-                nc.scalar.copy(out=raw, in_=bank[:])
-                nc.gpsimd.tensor_tensor(tile[:], raw, wg2_sb[:], ALU.mult)
-            else:
-                nc.scalar.copy(out=tile[:], in_=bank[:])
-            h2_sb[c] = tile
+            h2_sb[c] = ring.tile([P, S], F32, name="h2_sb", tag="h2_sb", bufs=STAGED)
+            nc.scalar.copy(out=h2_sb[c][:], in_=bank[:])
 
         def place_a(c):
-            nc.vector.tensor_copy(pages_a[c % PAGES][:].indirect(offs3_sb[:]), h1_sb[c][:])
+            nc.vector.tensor_tensor(pages_a[c % PAGES][:].indirect(offs3_sb[:]), h1_sb[c][:], wg1_abs[:], ALU.mult)
 
         def place_b(c):
-            if c >= HEAD_TILES:
-                nc.vector.tensor_copy(pages_b[c % PAGES][:].indirect(offs4_sb[:]), h2_sb[c][:])
-            else:
-                nc.vector.tensor_tensor(pages_b[c % PAGES][:].indirect(offs4_sb[:]), h2_sb[c][:], wg2_sb[:], ALU.mult)
+            nc.vector.tensor_tensor(pages_b[c % PAGES][:].indirect(offs4_sb[:]), h2_sb[c][:], wg2_sb[:], ALU.mult)
 
-        z_t = {}
 
-        def add_turned(c, term, h, start, stop):
+        def boost(c, cols):
+            nc.vector.scalar_tensor_tensor(
+                out=boosted[c % PAGES][:, cols], in0=pages_a[c % PAGES][:, cols], scalar=1.0, in1=vis_sb[c][:, cols],
+                op0=ALU.add, op1=ALU.mult,
+            )
+
+        def add_turned(c, term, h, first):
             for mb in range(M_BLOCKS):
                 nc.tensor.matmul(
                     sum_banks(c)[h][:, mb * P : (mb + 1) * P],
                     lhsT=term[:, h * BANK + mb * P : h * BANK + (mb + 1) * P], rhs=ident[:], is_transpose=True,
-                    start=(start and mb == 0), stop=(stop and mb == M_BLOCKS - 1),
+                    start=(first and mb == 0), stop=(not first and mb == M_BLOCKS - 1),
                 )
 
-        def scale_vis(c):
-            nc.gpsimd.tensor_tensor(scratch(c)[:], pages_a[c % PAGES][:], vis_sb[c][:], ALU.mult)
-
         def combine(c):
-            b, quad = divmod(c, TILES_PER_PASS)
+            quad = c % TILES_PER_PASS
             last = c == TILES - 1
             if last:
                 for h in range(HALVES):
-                    add_turned(c, pages_b[c % PAGES], h, True, False)
-                    cols = slice(h * BANK, (h + 1) * BANK)
-                    nc.vector.scalar_tensor_tensor(
-                        out=boost[c - 1][:, cols], in0=pages_a[c % PAGES][:, cols], scalar=1.0, in1=vis_sb[c][:, cols],
-                        op0=ALU.add, op1=ALU.mult,
-                    )
-                    add_turned(c, boost[c - 1], h, False, True)
+                    add_turned(c, pages_b[c % PAGES], h, True)
+                    boost(c, slice(h * BANK, (h + 1) * BANK))
+                    add_turned(c, boosted[c % PAGES], h, False)
             else:
-                for i, term in enumerate((vis_sb[c], boost[c], pages_b[c % PAGES])):
-                    for h in range(HALVES):
-                        add_turned(c, term, h, i == 0, i == 2)
+                boost(c, slice(0, T2))
+                for h in range(HALVES):
+                    add_turned(c, pages_b[c % PAGES], h, True)
+                for h in range(HALVES):
+                    add_turned(c, boosted[c % PAGES], h, False)
             for h in range(HALVES):
                 if quad == 0:
-                    z_t[h] = ring.tile([P, M_BLOCKS * K_PASS], BF16, name=f"z_t{h}", tag=f"z_t{h}")
-                bank = sum_banks(c)[h]
+                    z_t[h] = ring.tile([P, M_BLOCKS * PASS], BF16, name=f"z_t{h}", tag=f"z_t{h}")
+                dst = z_t[h][:].rearrange("m (mb u t q e) -> m mb u t q e", mb=M_BLOCKS, u=2, t=TILES_PER_PASS, e=2)
+                src = sum_banks(c)[h][:].rearrange("m (mb q u e) -> m mb u q e", mb=M_BLOCKS, u=2, e=2)
                 copy = nc.vector.tensor_copy if last and h == 1 else nc.scalar.copy
-                copy(
-                    out=z_t[h][:].rearrange("m (mb u t q e) -> m mb u t q e", mb=M_BLOCKS, u=2, t=TILES_PER_PASS, e=2)[:, :, :, quad, :, :],
-                    in_=bank[:].rearrange("m (mb q u e) -> m mb u q e", mb=M_BLOCKS, u=2, e=2),
-                )
+                copy(out=dst[:, :, :, quad, :, :], in_=src)
 
-        z_bf = {}
-        z_q = {}
-        w3_q = []
-
-        def turn_z(b):
+        def quantise_z(b):
             last = b == R_PASSES - 1
             grouped = ring.tile([P, T2 * PACK], BF16, name="z_bf", tag="z_bf", bufs=1, align_bytes=64)
             pairs = grouped[:].bitcast(F32).rearrange("p (m u) -> p m u", u=2)
@@ -296,14 +242,13 @@ def tile_list_alert_queue_ranker_kernel(
                     m0 = h * BANK + 2 * i * P
                     copy(out=pairs[:, m0 : m0 + 2 * P, :], in_=bank[:].rearrange("p (u m) -> p m u", u=2))
                 if last:
-                    lo, hi = h * BANK, (h + 1) * BANK
-                    z_q[b, h] = [plane[:] for plane in quantise(f"z_q{b}{h}", grouped[:, PACK * lo : PACK * hi])]
-            z_bf[b] = grouped
+                    codes, plane = quantise(f"z_q{b}{h}", grouped[:, PACK * h * BANK : PACK * (h + 1) * BANK])
+                    z_q[b, h] = (codes[:], plane[:])
+            if not last:
+                codes, plane = quantise(f"z_q{b}", grouped[:])
+                for h in range(HALVES):
+                    z_q[b, h] = (codes[:, h * BANK : (h + 1) * BANK], plane[:, h * BANK : (h + 1) * BANK])
 
-        def quantise_z(b):
-            planes = quantise(f"z_q{b}", z_bf[b][:])
-            for h in range(HALVES):
-                z_q[b, h] = [plane[:, h * BANK : (h + 1) * BANK] for plane in planes]
 
         def read_queue(pair, n, h, passes):
             for b in passes:
@@ -313,19 +258,48 @@ def tile_list_alert_queue_ranker_kernel(
                     rhs=z_q[b, h][0].bitcast(FP8X4), rhs_scale=z_q[b, h][1], start=(b == 0), stop=(b == R_PASSES - 1),
                 )
             for b in passes:
-                col = b * N + n * P
+                part, col = divmod(b * N + n * P, W3_CUT)
+                codes, plane = w3_q[part]
                 nc.tensor.matmul_mx(
-                    out=pair[0][:], lhsT=w3_q[col // W3_CUT][0][:, col % W3_CUT : col % W3_CUT + P].bitcast(FP8X4),
-                    lhsT_scale=w3_q[col // W3_CUT][1][:, col % W3_CUT : col % W3_CUT + P],
+                    out=pair[0][:], lhsT=codes[:, col : col + P].bitcast(FP8X4), lhsT_scale=plane[:, col : col + P],
                     rhs=z_q[b, h][0].bitcast(FP8X4), rhs_scale=z_q[b, h][1], start=(b == 0), stop=(b == R_PASSES - 1),
                 )
 
         def finish(pair, n, h):
             y2 = ring.tile([P, BANK], F32, name="y2", tag="y2")
             nc.scalar.copy(out=y2[:], in_=pair[1][:])
-            res = ring.tile([P, BANK], F32, name="res", tag="res", bufs=3)
+            res = ring.tile([P, BANK], F32, name="res", tag="res", bufs=N_TILES)
             nc.vector.tensor_tensor(res[:], pair[0][:], y2[:], ALU.mult)
             nc.sync.dma_start(out=out[n * P : (n + 1) * P, h * BANK : (h + 1) * BANK], in_=res[:])
+
+        make_identity(nc, ident[:])
+        for plane in (tab2_s, w2_s, tab_s):
+            nc.vector.memset(plane[:].bitcast(I32), 0)
+        for page in pages_b:
+            nc.vector.memset(page[:], 0.0)
+        nc.vector.memset(w4_s[:].bitcast(I32), 0)
+        nc.vector.memset(gain_rows[:], 0.0)
+
+        nc.sync.dma_start(offs2_sb[:], offs2)
+        load_w2(0, 1)
+        nc.sync.dma_start(offs_sb[:], offs)
+        load_table(tab2_w, tab2_words, 0)
+        load_plane(tab2_s, tab2_scales)
+        load_plane(w2_s, w2_scales)
+        load_plane(tab_s, tab_scales)
+        nc.gpsimd.dma_start(out=gain_rows[:TILES, :], in_=gain.rearrange("(c p) -> c p", p=P))
+        nc.sync.dma_start(out=wg2_sb[:], in_=wg2)
+        nc.sync.dma_start(offs4_sb[:], offs4)
+        load_table(tab_w[0], tab_words, 0)
+        load_w1(0)
+        load_table(tab_w[1], tab_words, 1)
+        load_w2(1, 2)
+        nc.sync.dma_start(out=wg1_sb[:], in_=wg1)
+        nc.sync.dma_start(offs3_sb[:], offs3)
+        load_w1(1)
+        load_w2(2, TILES)
+        load_vis(0)
+        load_w1(2)
 
         nc.vector.tensor_copy(v2_s[:], tab2_s[:].indirect(offs2_sb[:]))
         nc.vector.tensor_copy(v2_w[:], tab2_w[:].bitcast(U32).indirect(offs2_sb[:]))
@@ -334,86 +308,53 @@ def tile_list_alert_queue_ranker_kernel(
             nc.vector.memset(page[:], 0.0)
         nc.vector.tensor_copy(v_s[:], tab_s[:].indirect(offs_sb[:]))
         place_b(0)
-        round_w1(0)
-        quantise_w1(0)
+        prepare_w1(0)
         for a in range(K_PASSES):
             nc.vector.tensor_copy(v_w[a][:], tab_w[a][:].bitcast(U32).indirect(offs_sb[:]))
-        nc.tensor.transpose(banks[6][:, :P], gain_rows[:], ident[:])
-        nc.scalar.copy(out=gain_sb[:], in_=banks[6][:, :TILES])
+        nc.tensor.transpose(turn_banks[0][:, :P], gain_rows[:], ident[:])
+        nc.scalar.copy(out=gain_sb[:], in_=turn_banks[0][:, :TILES])
         stage_h2(1)
+        nc.scalar.activation(out=wg1_abs[:], in_=wg1_sb[:], func=ACT.Abs)
         stage_h1(0)
-        round_w1(1)
-        quantise_w1(1)
+        prepare_w1(1)
         stage_h1(1)
         place_b(1)
         load_vis(1)
-        load_w1(3)
-
-        def load_second_stage():
-            for b in range(R_PASSES):
-                load_w3(b)
-            nc.sync.dma_start(
-                out=w4_w[:].bitcast(I32).rearrange("p (a n) -> p a n", a=R_PASSES),
-                in_=w4_words.bitcast(I32).rearrange("a p n -> p a n"),
-            )
-            for q in range(QUADS):
-                nc.sync.dma_start(
-                    out=w4_s[32 * q : 32 * q + 4, :].bitcast(I32).rearrange("r (a n) -> r a n", a=R_PASSES),
-                    in_=w4_scales[:, 4 * q : 4 * q + 4, :].bitcast(I32).rearrange("a r n -> r a n"),
-                )
-
+        load_w1(RAW_BUFS)
         place_a(0)
-        place_a(1)
 
-        held_pairs = ((banks[4], banks[5]), (banks[0], banks[1]), (banks[2], banks[3]))
         for c in range(TILES):
-            if c + 2 < TILES:
-                stage_h1(c + 2)
-                stage_h2(c + 2)
-            if c < TILES - 1:
-                scale_vis(c)
-            if c + 2 < TILES:
-                place_a(c + 2)
-            if c == 2:
-                quantise_w1(3)
-            if c == 3:
-                quantise_w1(4)
-            if c == 5:
-                quantise_z(0)
-                w3_bf = round_weight([w3_raw[b] for b in range(R_PASSES)], "w3_bf", 1)
-            if c == 6:
-                w3_q.append(quantise("w3_q0", w3_bf[:, : PACK * W3_CUT]))
-            if c == 7:
-                w3_q.append(quantise("w3_q1", w3_bf[:, PACK * W3_CUT :]))
-            if c == 8:
-                quantise_z(1)
+            if c + AHEAD < TILES:
+                stage_h1(c + AHEAD)
+                stage_h2(c + AHEAD)
+            if c + 1 < TILES:
+                place_a(c + 1)
             if c == TILES - 1:
                 for n in range(N_TILES):
                     read_queue(held_pairs[n], n, 0, range(R_PASSES - 1))
             combine(c)
-            if c + 2 < TILES:
-                place_b(c + 2)
+            if 1 <= c < TILES - 1:
+                place_b(c + 1)
+            chunk = c + 2
+            if chunk < W1_CHUNKS:
+                prepare_w1(chunk)
+            if chunk + 2 < W1_CHUNKS:
+                load_w1(chunk + 2)
             if c == 0:
-                round_w1(2)
-                quantise_w1(2)
-                load_w1(4)
-                load_vis(2)
-                round_w1(3)
-                load_w1(5)
-                load_vis(3)
-            if c == 1:
-                round_w1(4)
-            if c + 4 < TILES:
-                load_vis(c + 4)
-            if c == 1:
+                for ahead in range(2, VIS_AHEAD):
+                    load_vis(ahead)
+            if c + VIS_AHEAD < TILES:
+                load_vis(c + VIS_AHEAD)
+            if chunk == W1_CHUNKS - 1:
                 load_second_stage()
             if c % TILES_PER_PASS == TILES_PER_PASS - 1:
-                turn_z(c // TILES_PER_PASS)
+                quantise_z(c // TILES_PER_PASS)
+            if chunk == W1_CHUNKS + 1:
+                prepare_w3()
 
         for n in range(N_TILES):
             read_queue(held_pairs[n], n, 0, [R_PASSES - 1])
             finish(held_pairs[n], n, 0)
-        late_pairs = (turn_banks, held_pairs[0], held_pairs[1])
         for n in range(N_TILES):
             read_queue(late_pairs[n], n, 1, range(R_PASSES))
             finish(late_pairs[n], n, 1)

@@ -30,11 +30,13 @@ HALVES = T2 // BANK
 M_BLOCKS = BANK // P
 N_TILES = N // P
 W1_COLS = 2 * P
-W1_CHUNKS = H // W1_COLS
+W1_GROUPS = ((0,), (1,), (2, 3), (4, 5))
 W3_CUT = 1024
 AHEAD = 2
 PAGES = 2
+SCRATCH = 3
 STAGED = AHEAD + 1
+LAST_ON_GPSIMD = TILES - 2
 RAW_BUFS = 3
 VIS_AHEAD = 4
 
@@ -77,17 +79,15 @@ def tile_list_alert_queue_ranker_kernel(
         w4_w = keep.tile([P, R_PASSES * 2 * N], U8, name="w4_w", align_bytes=64)
         w4_s = keep.tile([P, R_PASSES * N], U8, name="w4_s", align_bytes=64)
         wg1_sb = keep.tile([P, S], F32, name="wg1_sb")
-        wg1_abs = keep.tile([P, S], F32, name="wg1_abs")
         wg2_sb = keep.tile([P, S], F32, name="wg2_sb")
         gain_rows = keep.tile([P, P], F32, name="gain_rows")
         gain_sb = keep.tile([P, TILES], F32, name="gain_sb")
         ident = keep.tile([P, P], F32, name="ident")
         pages_a = [keep.tile([P, T2], F32, name=f"page_a{i}") for i in range(PAGES)]
         pages_b = [keep.tile([P, T2], F32, name=f"page_b{i}") for i in range(PAGES)]
-        boosted = [keep.tile([P, T2], F32, name=f"boosted{i}") for i in range(PAGES)]
 
         w1_raw, w3_raw, vis_sb, h1_sb, h2_sb = {}, {}, {}, {}, {}
-        w1_q, z_t, z_q = {}, {}, {}
+        w1_bf, w1_q, z_t, z_bf, z_q, scratch_sb = {}, {}, {}, {}, {}, {}
         w3_q = []
 
 
@@ -115,7 +115,7 @@ def tile_list_alert_queue_ranker_kernel(
             w1_raw[k] = raw
 
         def load_vis(c):
-            vis_sb[c] = ring.tile([P, T2], F32, name="vis_sb", tag="vis_sb", bufs=VIS_AHEAD + 1)
+            vis_sb[c] = ring.tile([P, T2], F32, name="vis_sb", tag="vis_sb", bufs=VIS_AHEAD)
             nc.sync.dma_start(out=vis_sb[c][:], in_=vis[c * P : (c + 1) * P, :])
 
         def load_second_stage():
@@ -141,25 +141,37 @@ def tile_list_alert_queue_ranker_kernel(
             for part in (slice(0, half), slice(half, 2 * half)):
                 nc.scalar.copy(out=dst[:, part], in_=src[:, part])
 
-        def quantise(name, grouped):
-            words = grouped.shape[1] // PACK
-            codes = keep.tile([P, words], U32, name=name, align_bytes=64)
-            plane = keep.tile([P, words], U8, name=name + "s", align_bytes=64)
-            nc.vector.quantize_mx(out=codes[:].bitcast(FP8X4), scales=plane[:], in_=grouped)
-            return codes, plane
+        def quantise(name, grouped, codes):
+            plane = keep.tile([P, codes.shape[1]], U8, name=name + "s", align_bytes=64)
+            nc.vector.quantize_mx(out=codes.bitcast(FP8X4), scales=plane[:], in_=grouped)
+            return codes, plane[:]
 
-        def prepare_w1(k):
-            grouped = ring.tile([P, PACK * K_PASSES * W1_COLS], BF16, name="w1_bf", tag="w1_bf", align_bytes=64)
-            round_weight(grouped[:], w1_raw[k])
-            w1_q[k] = quantise(f"w1_q{k}", grouped[:])
+        def own_codes(name, words):
+            return keep.tile([P, words], U32, name=name, align_bytes=64)[:]
 
-        def prepare_w3():
-            grouped = keep.tile([P, R_PASSES * PACK * N], BF16, name="w3_bf", align_bytes=64)
-            for b in range(R_PASSES):
-                round_weight(grouped[:, b * PACK * N : (b + 1) * PACK * N], w3_raw[b])
-            w3_q.append(quantise("w3_q0", grouped[:, : PACK * W3_CUT]))
-            w3_q.append(quantise("w3_q1", grouped[:, PACK * W3_CUT :]))
+        def round_w1(g):
+            width = PACK * K_PASSES * W1_COLS
+            w1_bf[g] = ring.tile([P, len(W1_GROUPS[g]) * width], BF16, name="w1_bf", tag="w1_bf", align_bytes=64)
+            for n, k in enumerate(W1_GROUPS[g]):
+                round_weight(w1_bf[g][:, n * width : (n + 1) * width], w1_raw[k])
 
+        def quantise_w1(g):
+            words = K_PASSES * W1_COLS
+            codes, plane = quantise(f"w1_q{g}", w1_bf[g][:], own_codes(f"w1_q{g}", len(W1_GROUPS[g]) * words))
+            for n, k in enumerate(W1_GROUPS[g]):
+                w1_q[k] = (codes[:, n * words : (n + 1) * words], plane[:, n * words : (n + 1) * words])
+
+
+        def scratch(c):
+            if c not in scratch_sb:
+                scratch_sb[c] = ring.tile([P, T2], F32, name="scratch", tag="scratch", bufs=SCRATCH)
+            return scratch_sb[c]
+
+        def unweighted(c, which):
+            return scratch(c - 1)[:].rearrange("p (h w x) -> p h w x", h=HALVES, w=2)[:, :, which, :]
+
+        def halves(ap):
+            return ap.rearrange("p (h x) -> p h x", h=HALVES)
 
         def stage_h1(c):
             bank = h1_banks[c % 2]
@@ -173,7 +185,9 @@ def tile_list_alert_queue_ranker_kernel(
                     start=(a == 0), stop=(a == K_PASSES - 1),
                 )
             h1_sb[c] = ring.tile([P, S], F32, name="h1_sb", tag="h1_sb", bufs=STAGED)
-            nc.scalar.activation(out=h1_sb[c][:], in_=bank[:], func=ACT.Tanh)
+            raw = unweighted(c, 0) if c > 0 else halves(h1_sb[c][:])
+            nc.scalar.activation(out=raw, in_=halves(bank[:]), func=ACT.Tanh)
+            nc.gpsimd.tensor_tensor(halves(h1_sb[c][:]), raw, halves(wg1_sb[:]), ALU.mult)
             nc.scalar.activation(out=h1_sb[c][:], in_=h1_sb[c][:], func=ACT.Abs, scale=gain_sb[:, c : c + 1])
 
         def stage_h2(c):
@@ -182,28 +196,37 @@ def tile_list_alert_queue_ranker_kernel(
                 out=bank[:], lhsT=w2_w[:, 2 * P * c : 2 * P * (c + 1)].bitcast(FP4X4), lhsT_scale=w2_s[:, c * P : (c + 1) * P],
                 rhs=v2_w[:].bitcast(FP8X4), rhs_scale=v2_s[:], start=True, stop=True,
             )
-            h2_sb[c] = ring.tile([P, S], F32, name="h2_sb", tag="h2_sb", bufs=STAGED)
-            nc.scalar.copy(out=h2_sb[c][:], in_=bank[:])
+            if c == LAST_ON_GPSIMD:
+                h2_sb[c] = ring.tile([P, S], F32, name="h2_late", tag="late", bufs=1, align_bytes=64)
+            else:
+                h2_sb[c] = ring.tile([P, S], F32, name="h2_sb", tag="h2_sb", bufs=STAGED)
+            if c == 0:
+                nc.scalar.copy(out=h2_sb[c][:], in_=bank[:])
+            else:
+                nc.scalar.copy(out=unweighted(c, 1), in_=halves(bank[:]))
+                nc.gpsimd.tensor_tensor(halves(h2_sb[c][:]), unweighted(c, 1), halves(wg2_sb[:]), ALU.mult)
 
         def place_a(c):
-            nc.vector.tensor_tensor(pages_a[c % PAGES][:].indirect(offs3_sb[:]), h1_sb[c][:], wg1_abs[:], ALU.mult)
+            nc.vector.tensor_copy(pages_a[c % PAGES][:].indirect(offs3_sb[:]), h1_sb[c][:])
 
         def place_b(c):
-            nc.vector.tensor_tensor(pages_b[c % PAGES][:].indirect(offs4_sb[:]), h2_sb[c][:], wg2_sb[:], ALU.mult)
+            if c == 0:
+                nc.vector.tensor_tensor(pages_b[0][:].indirect(offs4_sb[:]), h2_sb[c][:], wg2_sb[:], ALU.mult)
+            else:
+                nc.vector.tensor_copy(pages_b[c % PAGES][:].indirect(offs4_sb[:]), h2_sb[c][:])
 
 
-        def boost(c, cols):
-            nc.vector.scalar_tensor_tensor(
-                out=boosted[c % PAGES][:, cols], in0=pages_a[c % PAGES][:, cols], scalar=1.0, in1=vis_sb[c][:, cols],
-                op0=ALU.add, op1=ALU.mult,
-            )
+        def scale_vis(c):
+            for h in range(HALVES):
+                cols = slice(h * BANK, (h + 1) * BANK)
+                nc.gpsimd.tensor_tensor(scratch(c)[:, cols], pages_a[c % PAGES][:, cols], vis_sb[c][:, cols], ALU.mult)
 
-        def add_turned(c, term, h, first):
+        def add_turned(c, term, h, first, final):
             for mb in range(M_BLOCKS):
                 nc.tensor.matmul(
                     sum_banks(c)[h][:, mb * P : (mb + 1) * P],
                     lhsT=term[:, h * BANK + mb * P : h * BANK + (mb + 1) * P], rhs=ident[:], is_transpose=True,
-                    start=(first and mb == 0), stop=(not first and mb == M_BLOCKS - 1),
+                    start=(first and mb == 0), stop=(final and mb == M_BLOCKS - 1),
                 )
 
         def combine(c):
@@ -211,15 +234,18 @@ def tile_list_alert_queue_ranker_kernel(
             last = c == TILES - 1
             if last:
                 for h in range(HALVES):
-                    add_turned(c, pages_b[c % PAGES], h, True)
-                    boost(c, slice(h * BANK, (h + 1) * BANK))
-                    add_turned(c, boosted[c % PAGES], h, False)
+                    cols = slice(h * BANK, (h + 1) * BANK)
+                    add_turned(c, pages_b[c % PAGES], h, True, False)
+                    nc.vector.scalar_tensor_tensor(
+                        out=scratch(c - 1)[:, cols], in0=pages_a[c % PAGES][:, cols], scalar=1.0, in1=vis_sb[c][:, cols],
+                        op0=ALU.add, op1=ALU.mult,
+                    )
+                    add_turned(c, scratch(c - 1), h, False, True)
             else:
-                boost(c, slice(0, T2))
-                for h in range(HALVES):
-                    add_turned(c, pages_b[c % PAGES], h, True)
-                for h in range(HALVES):
-                    add_turned(c, boosted[c % PAGES], h, False)
+                terms = (vis_sb[c], scratch(c), pages_b[c % PAGES])
+                for i, term in enumerate(terms):
+                    for h in range(HALVES):
+                        add_turned(c, term, h, i == 0, i == len(terms) - 1)
             for h in range(HALVES):
                 if quad == 0:
                     z_t[h] = ring.tile([P, M_BLOCKS * PASS], BF16, name=f"z_t{h}", tag=f"z_t{h}")
@@ -228,9 +254,9 @@ def tile_list_alert_queue_ranker_kernel(
                 copy = nc.vector.tensor_copy if last and h == 1 else nc.scalar.copy
                 copy(out=dst[:, :, :, quad, :, :], in_=src)
 
-        def quantise_z(b):
+        def turn_z(b):
             last = b == R_PASSES - 1
-            grouped = ring.tile([P, T2 * PACK], BF16, name="z_bf", tag="z_bf", bufs=1, align_bytes=64)
+            grouped = ring.tile([P, T2 * PACK], BF16, name="z_bf", tag="z_bf", align_bytes=64)
             pairs = grouped[:].bitcast(F32).rearrange("p (m u) -> p m u", u=2)
             for h in range(HALVES):
                 words = z_t[h][:].bitcast(F32).rearrange("m (mb u p) -> m mb u p", mb=M_BLOCKS, u=2)
@@ -242,12 +268,22 @@ def tile_list_alert_queue_ranker_kernel(
                     m0 = h * BANK + 2 * i * P
                     copy(out=pairs[:, m0 : m0 + 2 * P, :], in_=bank[:].rearrange("p (u m) -> p m u", u=2))
                 if last:
-                    codes, plane = quantise(f"z_q{b}{h}", grouped[:, PACK * h * BANK : PACK * (h + 1) * BANK])
-                    z_q[b, h] = (codes[:], plane[:])
-            if not last:
-                codes, plane = quantise(f"z_q{b}", grouped[:])
-                for h in range(HALVES):
-                    z_q[b, h] = (codes[:, h * BANK : (h + 1) * BANK], plane[:, h * BANK : (h + 1) * BANK])
+                    name = f"z_q{b}{h}"
+                    z_q[b, h] = quantise(name, grouped[:, PACK * h * BANK : PACK * (h + 1) * BANK], own_codes(name, BANK))
+            z_bf[b] = grouped
+
+        def quantise_z(b, codes):
+            codes, plane = quantise(f"z_q{b}", z_bf[b][:], codes)
+            for h in range(HALVES):
+                z_q[b, h] = (codes[:, h * BANK : (h + 1) * BANK], plane[:, h * BANK : (h + 1) * BANK])
+
+        def quantise_second_stage(w3_bf):
+            w3_words = R_PASSES * N
+            late = ring.tile([P, 2 * T2 + w3_words], U32, name="late", tag="late", bufs=1, align_bytes=64)
+            quantise_z(0, late[:, T2 + w3_words :])
+            w3_q.append(quantise("w3_q0", w3_bf[:, : PACK * W3_CUT], late[:, T2 : T2 + W3_CUT]))
+            w3_q.append(quantise("w3_q1", w3_bf[:, PACK * W3_CUT :], late[:, T2 + W3_CUT : T2 + w3_words]))
+            quantise_z(1, late[:, :T2])
 
 
         def read_queue(pair, n, h, passes):
@@ -292,13 +328,13 @@ def tile_list_alert_queue_ranker_kernel(
         nc.sync.dma_start(offs4_sb[:], offs4)
         load_table(tab_w[0], tab_words, 0)
         load_w1(0)
-        load_table(tab_w[1], tab_words, 1)
         load_w2(1, 2)
+        load_table(tab_w[1], tab_words, 1)
         nc.sync.dma_start(out=wg1_sb[:], in_=wg1)
         nc.sync.dma_start(offs3_sb[:], offs3)
-        load_w1(1)
         load_w2(2, TILES)
         load_vis(0)
+        load_w1(1)
         load_w1(2)
 
         nc.vector.tensor_copy(v2_s[:], tab2_s[:].indirect(offs2_sb[:]))
@@ -308,49 +344,60 @@ def tile_list_alert_queue_ranker_kernel(
             nc.vector.memset(page[:], 0.0)
         nc.vector.tensor_copy(v_s[:], tab_s[:].indirect(offs_sb[:]))
         place_b(0)
-        prepare_w1(0)
+        round_w1(0)
+        quantise_w1(0)
         for a in range(K_PASSES):
             nc.vector.tensor_copy(v_w[a][:], tab_w[a][:].bitcast(U32).indirect(offs_sb[:]))
         nc.tensor.transpose(turn_banks[0][:, :P], gain_rows[:], ident[:])
         nc.scalar.copy(out=gain_sb[:], in_=turn_banks[0][:, :TILES])
         stage_h2(1)
-        nc.scalar.activation(out=wg1_abs[:], in_=wg1_sb[:], func=ACT.Abs)
         stage_h1(0)
-        prepare_w1(1)
+        round_w1(1)
+        quantise_w1(1)
         stage_h1(1)
         place_b(1)
         load_vis(1)
         load_w1(RAW_BUFS)
         place_a(0)
+        place_a(1)
+        w3_bf = keep.tile([P, R_PASSES * PACK * N], BF16, name="w3_bf", align_bytes=64)
 
         for c in range(TILES):
             if c + AHEAD < TILES:
                 stage_h1(c + AHEAD)
                 stage_h2(c + AHEAD)
-            if c + 1 < TILES:
-                place_a(c + 1)
+            if c <= LAST_ON_GPSIMD:
+                scale_vis(c)
+            if c + AHEAD < TILES:
+                place_a(c + AHEAD)
+            if c == 3:
+                quantise_w1(3)
+            if c == 5:
+                for b in range(R_PASSES):
+                    round_weight(w3_bf[:, b * PACK * N : (b + 1) * PACK * N], w3_raw[b])
             if c == TILES - 1:
                 for n in range(N_TILES):
                     read_queue(held_pairs[n], n, 0, range(R_PASSES - 1))
             combine(c)
-            if 1 <= c < TILES - 1:
-                place_b(c + 1)
-            chunk = c + 2
-            if chunk < W1_CHUNKS:
-                prepare_w1(chunk)
-            if chunk + 2 < W1_CHUNKS:
-                load_w1(chunk + 2)
+            if c + AHEAD < TILES:
+                place_b(c + AHEAD)
+            if c + AHEAD == LAST_ON_GPSIMD:
+                quantise_second_stage(w3_bf)
             if c == 0:
-                for ahead in range(2, VIS_AHEAD):
-                    load_vis(ahead)
+                load_w1(4)
+                load_vis(2)
+                round_w1(2)
+                quantise_w1(2)
+                load_w1(5)
+                load_vis(3)
+            if c == 1:
+                round_w1(3)
             if c + VIS_AHEAD < TILES:
                 load_vis(c + VIS_AHEAD)
-            if chunk == W1_CHUNKS - 1:
+            if c == 1:
                 load_second_stage()
             if c % TILES_PER_PASS == TILES_PER_PASS - 1:
-                quantise_z(c // TILES_PER_PASS)
-            if chunk == W1_CHUNKS + 1:
-                prepare_w3()
+                turn_z(c // TILES_PER_PASS)
 
         for n in range(N_TILES):
             read_queue(held_pairs[n], n, 0, [R_PASSES - 1])

from contextlib import ExitStack

import concourse.mybir as mybir
from concourse.masks import make_identity

K, K2, T, S, T2, H, N = 1024, 512, 2048, 512, 1024, 1536, 384
FLOPS = 2 * (K * H * S + K2 * H * S + 2 * H * N * T2)

F32 = mybir.dt.float32
BF16 = mybir.dt.bfloat16
I32 = mybir.dt.int32
U32 = mybir.dt.uint32
U16 = mybir.dt.uint16
U8 = mybir.dt.uint8
FP8X4 = mybir.dt.float8_e4m3fn_x4
FP4X4 = mybir.dt.float4_e2m1fn_x4
ALU = mybir.AluOpType
ACT = mybir.ActivationFunctionType

P = 128
PACK = 4
PASS = P * PACK
BANK = 512
QUADS = 4
TILES = H // P
TILES_PER_PASS = PASS // P
K_PASSES = K // PASS
R_PASSES = H // PASS
HALVES = T2 // BANK
M_BLOCKS = BANK // P
N_TILES = N // P
W1_COLS = 2 * P
W1_GROUPS = ((0,), (1,), (2, 3), (4, 5))
W3_CUT = 1024
AHEAD = 2
PAGES = 2
SCRATCH = 3
STAGED = AHEAD + 1
LAST_ON_GPSIMD = TILES - 2
RAW_BUFS = 3
VIS_AHEAD = 4


def tile_list_alert_queue_ranker_kernel(
    tc, tab_words, tab_scales, tab2_words, tab2_scales, offs, offs2, offs3, offs4,
    w1, gain, w2_words, w2_scales, wg1, wg2, vis, w3, w4_words, w4_scales, out,
):
    nc = tc.nc
    with ExitStack() as ctx:
        keep = ctx.enter_context(tc.tile_pool(name="keep", bufs=1))
        ring = ctx.enter_context(tc.tile_pool(name="ring", bufs=2))
        psum = ctx.enter_context(tc.psum_pool(name="psum", bufs=1))

        banks = [psum.tile([P, BANK], F32, name=f"bank{i}") for i in range(8)]
        h1_banks = (banks[0], banks[4])
        h2_banks = (banks[1], banks[5])
        even_banks = (banks[2], banks[3])
        turn_banks = (banks[6], banks[7])
        held_pairs = ((banks[4], banks[5]), (banks[0], banks[1]), even_banks)
        late_pairs = (turn_banks, held_pairs[0], held_pairs[1])

        def sum_banks(c):
            return even_banks if c % 2 == 0 and c < TILES - 2 else turn_banks

        offs_sb = keep.tile([P, S // 16], U16, name="offs_sb")
        offs2_sb = keep.tile([P, S // 16], U16, name="offs2_sb")
        offs3_sb = keep.tile([P, S // 16], U16, name="offs3_sb")
        offs4_sb = keep.tile([P, S // 16], U16, name="offs4_sb")
        tab_w = [keep.tile([P, T], I32, name=f"tab_w{a}", align_bytes=64) for a in range(K_PASSES)]
        tab_s = keep.tile([P, T], U8, name="tab_s", align_bytes=64)
        tab2_w = keep.tile([P, T], I32, name="tab2_w", align_bytes=64)
        tab2_s = keep.tile([P, T], U8, name="tab2_s", align_bytes=64)
        v_w = [keep.tile([P, S], U32, name=f"v_w{a}", align_bytes=64) for a in range(K_PASSES)]
        v_s = keep.tile([P, S], U8, name="v_s", align_bytes=64)
        v2_w = keep.tile([P, S], U32, name="v2_w", align_bytes=64)
        v2_s = keep.tile([P, S], U8, name="v2_s", align_bytes=64)
        w2_w = keep.tile([P, 2 * H], U8, name="w2_w", align_bytes=64)
        w2_s = keep.tile([P, H], U8, name="w2_s", align_bytes=64)
        w4_w = keep.tile([P, R_PASSES * 2 * N], U8, name="w4_w", align_bytes=64)
        w4_s = keep.tile([P, R_PASSES * N], U8, name="w4_s", align_bytes=64)
        wg1_sb = keep.tile([P, S], F32, name="wg1_sb")
        wg2_sb = keep.tile([P, S], F32, name="wg2_sb")
        gain_rows = keep.tile([P, P], F32, name="gain_rows")
        gain_sb = keep.tile([P, TILES], F32, name="gain_sb")
        ident = keep.tile([P, P], F32, name="ident")
        pages_a = [keep.tile([P, T2], F32, name=f"page_a{i}") for i in range(PAGES)]
        pages_b = [keep.tile([P, T2], F32, name=f"page_b{i}") for i in range(PAGES)]

        w1_raw, w3_raw, vis_sb, h1_sb, h2_sb = {}, {}, {}, {}, {}
        w1_bf, w1_q, z_t, z_bf, z_q, scratch_sb = {}, {}, {}, {}, {}, {}
        w3_q = []


        def load_plane(plane, scales):
            passes = scales.shape[0]
            for q in range(QUADS):
                nc.sync.dma_start(
                    out=plane[32 * q : 32 * q + 4 * passes, :].bitcast(I32),
                    in_=scales[:, 4 * q : 4 * q + 4, :].bitcast(I32),
                )

        def load_table(tile, words, a):
            nc.sync.dma_start(out=tile[:], in_=words[a].rearrange("p t i -> p (t i)").bitcast(I32))

        def load_w2(first, end):
            cols = slice(2 * P * first, 2 * P * end)
            nc.sync.dma_start(out=w2_w[:, cols].bitcast(I32), in_=w2_words[0][:, cols].bitcast(I32))

        def load_w1(k):
            raw = ring.tile([P, PACK * K_PASSES * W1_COLS], F32, name="w_raw", tag="w_raw", bufs=RAW_BUFS)
            view = raw[:].rearrange("p (j a c) -> p j a c", j=PACK, a=K_PASSES)
            for a in range(K_PASSES):
                rows = w1[a * PASS : (a + 1) * PASS, k * W1_COLS : (k + 1) * W1_COLS]
                nc.sync.dma_start(out=view[:, :, a, :], in_=rows.rearrange("(p j) c -> p j c", j=PACK))
            w1_raw[k] = raw

        def load_vis(c):
            vis_sb[c] = ring.tile([P, T2], F32, name="vis_sb", tag="vis_sb", bufs=VIS_AHEAD)
            nc.sync.dma_start(out=vis_sb[c][:], in_=vis[c * P : (c + 1) * P, :])

        def load_second_stage():
            for b in range(R_PASSES):
                w3_raw[b] = ring.tile([P, PACK * N], F32, name="w_raw", tag="w_raw", bufs=RAW_BUFS)
                rows = w3[b * PASS : (b + 1) * PASS, :]
                nc.sync.dma_start(out=w3_raw[b][:], in_=rows.rearrange("(p j) n -> p (j n)", j=PACK))
            nc.sync.dma_start(
                out=w4_w[:].bitcast(I32).rearrange("p (b n) -> p b n", b=R_PASSES),
                in_=w4_words.bitcast(I32).rearrange("b p n -> p b n"),
            )
            for q in range(QUADS):
                nc.sync.dma_start(
                    out=w4_s[32 * q : 32 * q + 4, :].bitcast(I32).rearrange("r (b n) -> r b n", b=R_PASSES),
                    in_=w4_scales[:, 4 * q : 4 * q + 4, :].bitcast(I32).rearrange("b r n -> r b n"),
                )


        def round_weight(grouped, raw):
            dst = grouped.rearrange("p (g i j) -> p g j i", i=4, j=PACK)
            src = raw[:].rearrange("p (j g i) -> p g j i", i=4, j=PACK)
            half = src.shape[1] // 2
            for part in (slice(0, half), slice(half, 2 * half)):
                nc.scalar.copy(out=dst[:, part], in_=src[:, part])

        def quantise(name, grouped, codes):
            plane = keep.tile([P, codes.shape[1]], U8, name=name + "s", align_bytes=64)
            nc.vector.quantize_mx(out=codes.bitcast(FP8X4), scales=plane[:], in_=grouped)
            return codes, plane[:]

        def own_codes(name, words):
            return keep.tile([P, words], U32, name=name, align_bytes=64)[:]

        def round_w1(g):
            width = PACK * K_PASSES * W1_COLS
            w1_bf[g] = ring.tile([P, len(W1_GROUPS[g]) * width], BF16, name="w1_bf", tag="w1_bf", align_bytes=64)
            for n, k in enumerate(W1_GROUPS[g]):
                round_weight(w1_bf[g][:, n * width : (n + 1) * width], w1_raw[k])

        def quantise_w1(g):
            words = K_PASSES * W1_COLS
            codes, plane = quantise(f"w1_q{g}", w1_bf[g][:], own_codes(f"w1_q{g}", len(W1_GROUPS[g]) * words))
            for n, k in enumerate(W1_GROUPS[g]):
                w1_q[k] = (codes[:, n * words : (n + 1) * words], plane[:, n * words : (n + 1) * words])


        def scratch(c):
            if c not in scratch_sb:
                scratch_sb[c] = ring.tile([P, T2], F32, name="scratch", tag="scratch", bufs=SCRATCH)
            return scratch_sb[c]

        def unweighted(c, which):
            return scratch(c - 1)[:].rearrange("p (h w x) -> p h w x", h=HALVES, w=2)[:, :, which, :]

        def halves(ap):
            return ap.rearrange("p (h x) -> p h x", h=HALVES)

        def stage_h1(c):
            bank = h1_banks[c % 2]
            k, col = divmod(c * P, W1_COLS)
            codes, plane = w1_q[k]
            for a in range(K_PASSES):
                cols = slice(a * W1_COLS + col, a * W1_COLS + col + P)
                nc.tensor.matmul_mx(
                    out=bank[:], lhsT=codes[:, cols].bitcast(FP8X4), lhsT_scale=plane[:, cols],
                    rhs=v_w[a][:].bitcast(FP8X4), rhs_scale=v_s[4 * a :, :],
                    start=(a == 0), stop=(a == K_PASSES - 1),
                )
            h1_sb[c] = ring.tile([P, S], F32, name="h1_sb", tag="h1_sb", bufs=STAGED)
            raw = unweighted(c, 0) if c > 0 else halves(h1_sb[c][:])
            nc.scalar.activation(out=raw, in_=halves(bank[:]), func=ACT.Tanh)
            nc.gpsimd.tensor_tensor(halves(h1_sb[c][:]), raw, halves(wg1_sb[:]), ALU.mult)
            nc.scalar.activation(out=h1_sb[c][:], in_=h1_sb[c][:], func=ACT.Abs, scale=gain_sb[:, c : c + 1])

        def stage_h2(c):
            bank = h2_banks[c % 2]
            nc.tensor.matmul_mx(
                out=bank[:], lhsT=w2_w[:, 2 * P * c : 2 * P * (c + 1)].bitcast(FP4X4), lhsT_scale=w2_s[:, c * P : (c + 1) * P],
                rhs=v2_w[:].bitcast(FP8X4), rhs_scale=v2_s[:], start=True, stop=True,
            )
            if c == LAST_ON_GPSIMD:
                h2_sb[c] = ring.tile([P, S], F32, name="h2_late", tag="late", bufs=1, align_bytes=64)
            else:
                h2_sb[c] = ring.tile([P, S], F32, name="h2_sb", tag="h2_sb", bufs=STAGED)
            if c == 0:
                nc.scalar.copy(out=h2_sb[c][:], in_=bank[:])
            else:
                nc.scalar.copy(out=unweighted(c, 1), in_=halves(bank[:]))
                nc.gpsimd.tensor_tensor(halves(h2_sb[c][:]), unweighted(c, 1), halves(wg2_sb[:]), ALU.mult)

        def place_a(c):
            nc.vector.tensor_copy(pages_a[c % PAGES][:].indirect(offs3_sb[:]), h1_sb[c][:])

        def place_b(c):
            if c == 0:
                nc.vector.tensor_tensor(pages_b[0][:].indirect(offs4_sb[:]), h2_sb[c][:], wg2_sb[:], ALU.mult)
            else:
                nc.vector.tensor_copy(pages_b[c % PAGES][:].indirect(offs4_sb[:]), h2_sb[c][:])


        def scale_vis(c):
            for h in range(HALVES):
                cols = slice(h * BANK, (h + 1) * BANK)
                nc.gpsimd.tensor_tensor(scratch(c)[:, cols], pages_a[c % PAGES][:, cols], vis_sb[c][:, cols], ALU.mult)

        def add_turned(c, term, h, first, final):
            for mb in range(M_BLOCKS):
                nc.tensor.matmul(
                    sum_banks(c)[h][:, mb * P : (mb + 1) * P],
                    lhsT=term[:, h * BANK + mb * P : h * BANK + (mb + 1) * P], rhs=ident[:], is_transpose=True,
                    start=(first and mb == 0), stop=(final and mb == M_BLOCKS - 1),
                )

        def combine(c):
            quad = c % TILES_PER_PASS
            last = c == TILES - 1
            if last:
                for h in range(HALVES):
                    cols = slice(h * BANK, (h + 1) * BANK)
                    add_turned(c, pages_b[c % PAGES], h, True, False)
                    nc.vector.scalar_tensor_tensor(
                        out=scratch(c - 1)[:, cols], in0=pages_a[c % PAGES][:, cols], scalar=1.0, in1=vis_sb[c][:, cols],
                        op0=ALU.add, op1=ALU.mult,
                    )
                    add_turned(c, scratch(c - 1), h, False, True)
            else:
                terms = (vis_sb[c], scratch(c), pages_b[c % PAGES])
                for i, term in enumerate(terms):
                    for h in range(HALVES):
                        add_turned(c, term, h, i == 0, i == len(terms) - 1)
            for h in range(HALVES):
                if quad == 0:
                    z_t[h] = ring.tile([P, M_BLOCKS * PASS], BF16, name=f"z_t{h}", tag=f"z_t{h}")
                dst = z_t[h][:].rearrange("m (mb u t q e) -> m mb u t q e", mb=M_BLOCKS, u=2, t=TILES_PER_PASS, e=2)
                src = sum_banks(c)[h][:].rearrange("m (mb q u e) -> m mb u q e", mb=M_BLOCKS, u=2, e=2)
                copy = nc.vector.tensor_copy if last and h == 1 else nc.scalar.copy
                copy(out=dst[:, :, :, quad, :, :], in_=src)

        def turn_z(b):
            last = b == R_PASSES - 1
            grouped = ring.tile([P, T2 * PACK], BF16, name="z_bf", tag="z_bf", align_bytes=64)
            pairs = grouped[:].bitcast(F32).rearrange("p (m u) -> p m u", u=2)
            for h in range(HALVES):
                words = z_t[h][:].bitcast(F32).rearrange("m (mb u p) -> m mb u p", mb=M_BLOCKS, u=2)
                for i, bank in enumerate(turn_banks):
                    for u in range(2):
                        for j in range(2):
                            nc.tensor.transpose(bank[:, (2 * u + j) * P : (2 * u + j + 1) * P], words[:, 2 * i + j, u, :], ident[:])
                    copy = nc.vector.tensor_copy if last and i == 1 else nc.scalar.copy
                    m0 = h * BANK + 2 * i * P
                    copy(out=pairs[:, m0 : m0 + 2 * P, :], in_=bank[:].rearrange("p (u m) -> p m u", u=2))
                if last:
                    name = f"z_q{b}{h}"
                    z_q[b, h] = quantise(name, grouped[:, PACK * h * BANK : PACK * (h + 1) * BANK], own_codes(name, BANK))
            z_bf[b] = grouped

        def quantise_z(b, codes):
            codes, plane = quantise(f"z_q{b}", z_bf[b][:], codes)
            for h in range(HALVES):
                z_q[b, h] = (codes[:, h * BANK : (h + 1) * BANK], plane[:, h * BANK : (h + 1) * BANK])

        def quantise_second_stage(w3_bf):
            w3_words = R_PASSES * N
            late = ring.tile([P, 2 * T2 + w3_words], U32, name="late", tag="late", bufs=1, align_bytes=64)
            quantise_z(0, late[:, T2 + w3_words :])
            w3_q.append(quantise("w3_q0", w3_bf[:, : PACK * W3_CUT], late[:, T2 : T2 + W3_CUT]))
            w3_q.append(quantise("w3_q1", w3_bf[:, PACK * W3_CUT :], late[:, T2 + W3_CUT : T2 + w3_words]))
            quantise_z(1, late[:, :T2])


        def read_queue(pair, n, h, passes):
            for b in passes:
                col = b * N + n * P
                nc.tensor.matmul_mx(
                    out=pair[1][:], lhsT=w4_w[:, 2 * col : 2 * (col + P)].bitcast(FP4X4), lhsT_scale=w4_s[:, col : col + P],
                    rhs=z_q[b, h][0].bitcast(FP8X4), rhs_scale=z_q[b, h][1], start=(b == 0), stop=(b == R_PASSES - 1),
                )
            for b in passes:
                part, col = divmod(b * N + n * P, W3_CUT)
                codes, plane = w3_q[part]
                nc.tensor.matmul_mx(
                    out=pair[0][:], lhsT=codes[:, col : col + P].bitcast(FP8X4), lhsT_scale=plane[:, col : col + P],
                    rhs=z_q[b, h][0].bitcast(FP8X4), rhs_scale=z_q[b, h][1], start=(b == 0), stop=(b == R_PASSES - 1),
                )

        def finish(pair, n, h):
            y2 = ring.tile([P, BANK], F32, name="y2", tag="y2")
            nc.scalar.copy(out=y2[:], in_=pair[1][:])
            res = ring.tile([P, BANK], F32, name="res", tag="res", bufs=N_TILES)
            nc.vector.tensor_tensor(res[:], pair[0][:], y2[:], ALU.mult)
            nc.sync.dma_start(out=out[n * P : (n + 1) * P, h * BANK : (h + 1) * BANK], in_=res[:])

        make_identity(nc, ident[:])
        for plane in (tab2_s, w2_s, tab_s):
            nc.vector.memset(plane[:].bitcast(I32), 0)
        for page in pages_b:
            nc.vector.memset(page[:], 0.0)
        nc.vector.memset(w4_s[:].bitcast(I32), 0)
        nc.vector.memset(gain_rows[:], 0.0)

        nc.sync.dma_start(offs2_sb[:], offs2)
        load_w2(0, 1)
        nc.sync.dma_start(offs_sb[:], offs)
        load_table(tab2_w, tab2_words, 0)
        load_plane(tab2_s, tab2_scales)
        load_plane(w2_s, w2_scales)
        load_plane(tab_s, tab_scales)
        nc.gpsimd.dma_start(out=gain_rows[:TILES, :], in_=gain.rearrange("(c p) -> c p", p=P))
        nc.sync.dma_start(out=wg2_sb[:], in_=wg2)
        nc.sync.dma_start(offs4_sb[:], offs4)
        load_table(tab_w[0], tab_words, 0)
        load_w1(0)
        load_w2(1, 2)
        load_table(tab_w[1], tab_words, 1)
        nc.sync.dma_start(out=wg1_sb[:], in_=wg1)
        nc.sync.dma_start(offs3_sb[:], offs3)
        load_w2(2, TILES)
        load_vis(0)
        load_w1(1)
        load_w1(2)

        nc.vector.tensor_copy(v2_s[:], tab2_s[:].indirect(offs2_sb[:]))
        nc.vector.tensor_copy(v2_w[:], tab2_w[:].bitcast(U32).indirect(offs2_sb[:]))
        stage_h2(0)
        for page in pages_a:
            nc.vector.memset(page[:], 0.0)
        nc.vector.tensor_copy(v_s[:], tab_s[:].indirect(offs_sb[:]))
        place_b(0)
        round_w1(0)
        quantise_w1(0)
        for a in range(K_PASSES):
            nc.vector.tensor_copy(v_w[a][:], tab_w[a][:].bitcast(U32).indirect(offs_sb[:]))
        nc.tensor.transpose(turn_banks[0][:, :P], gain_rows[:], ident[:])
        nc.scalar.copy(out=gain_sb[:], in_=turn_banks[0][:, :TILES])
        stage_h2(1)
        stage_h1(0)
        round_w1(1)
        quantise_w1(1)
        stage_h1(1)
        place_b(1)
        load_vis(1)
        load_w1(RAW_BUFS)
        place_a(0)
        place_a(1)
        w3_bf = keep.tile([P, R_PASSES * PACK * N], BF16, name="w3_bf", align_bytes=64)

        for c in range(TILES):
            if c + AHEAD < TILES:
                stage_h1(c + AHEAD)
                stage_h2(c + AHEAD)
            if c <= LAST_ON_GPSIMD:
                scale_vis(c)
            if c + AHEAD < TILES:
                place_a(c + AHEAD)
            if c == 3:
                quantise_w1(3)
            if c == 5:
                for b in range(R_PASSES):
                    round_weight(w3_bf[:, b * PACK * N : (b + 1) * PACK * N], w3_raw[b])
            if c == TILES - 1:
                for n in range(N_TILES):
                    read_queue(held_pairs[n], n, 0, range(R_PASSES - 1))
            combine(c)
            if c + AHEAD < TILES:
                place_b(c + AHEAD)
            if c + AHEAD == LAST_ON_GPSIMD:
                quantise_second_stage(w3_bf)
            if c == 0:
                load_w1(4)
                load_vis(2)
                round_w1(2)
                quantise_w1(2)
                load_w1(5)
                load_vis(3)
            if c == 1:
                round_w1(3)
            if c + VIS_AHEAD < TILES:
                load_vis(c + VIS_AHEAD)
            if c == 1:
                load_second_stage()
            if c % TILES_PER_PASS == TILES_PER_PASS - 1:
                turn_z(c // TILES_PER_PASS)

        for n in range(N_TILES):
            read_queue(held_pairs[n], n, 0, [R_PASSES - 1])
            finish(held_pairs[n], n, 0)
        for n in range(N_TILES):
            read_queue(late_pairs[n], n, 1, range(R_PASSES))
            finish(late_pairs[n], n, 1)
